import numpy as np
import ml_dtypes


def mxq(x, axis, fmt="e4m3"):
    dtype, down = {"e4m3": (ml_dtypes.float8_e4m3fn, 7), "e5m2": (ml_dtypes.float8_e5m2, 14)}[fmt]
    v = np.moveaxis(np.asarray(x, np.float32).astype(ml_dtypes.bfloat16).astype(np.float64), axis, -1)
    blocks = v.reshape(v.shape[:-1] + (-1, 32))
    amax = np.abs(blocks).max(-1, keepdims=True)
    byte = np.maximum(np.where(amax > 0, np.frexp(amax)[1] - 1 + 127, 0) - down, 1)
    scale = np.exp2(byte - 127.0)
    codes = (blocks / scale).astype(np.float32).astype(dtype).astype(np.float64)
    return np.moveaxis((codes * scale).reshape(v.shape), -1, axis)


WIDE = False


def mx_kscale(k):
    if not WIDE:
        return np.ones(k)
    levels = np.array([10, -10, 5, -5, 0])
    if k % 512:
        return np.exp2(np.random.permutation(np.resize(levels, k // 32))).repeat(32)
    a = np.empty((k // 512, 16))
    for p in range(k // 512):
        a[p, :8] = np.random.permutation(np.resize(levels, 8))
        for g in range(8):
            far = levels[np.abs(levels - a[p, g]) >= 10]
            a[p, g + 8] = far[np.random.randint(len(far))]
    return np.exp2(a.ravel()).repeat(32)


BF16 = ml_dtypes.bfloat16


def bf(x):
    return np.asarray(x, np.float32).astype(BF16)


def f64(x):
    return np.asarray(x).astype(np.float64)


E2M1 = np.array([0.0, 0.5, 1.0, 1.5, 2.0, 3.0, 4.0, 6.0, -0.0, -0.5, -1.0, -1.5, -2.0, -3.0, -4.0, -6.0])


def pack_weight(w, fmt):
    k, n = w.shape
    w = f64(bf(w)).reshape(k // 32, 32, n)
    amax = np.abs(w).max(1)
    if fmt == "e4m3":
        byte = np.frexp(amax)[1] - 1 + 127 - 7
    else:
        mant, ex = np.frexp(amax / 6.0)
        byte = np.where(mant > 0.5, ex, ex - 1) + 127
    byte = np.clip(np.where(amax > 0, byte, 1), 1, 254)
    scaled = (w * np.exp2(127.0 - byte)[:, None, :]).reshape(k, n).astype(np.float32)
    by_word = np.ascontiguousarray(scaled.reshape(k // 512, 128, 4, n).transpose(0, 1, 3, 2))
    if fmt == "e4m3":
        words = by_word.astype(ml_dtypes.float8_e4m3fn).view(np.uint8)
    else:
        c = by_word.astype(ml_dtypes.float4_e2m1fn).view(np.uint8) & 0xF
        words = c[..., 0::2] | (c[..., 1::2] << 4)
    return np.ascontiguousarray(words), np.ascontiguousarray(byte.astype(np.uint8).reshape(k // 512, 16, n))


def unpack_weight(words, scales, fmt):
    g, p, n, _ = words.shape
    if fmt == "e4m3":
        vals = np.ascontiguousarray(words).view(ml_dtypes.float8_e4m3fn).astype(np.float64)
    else:
        nib = np.empty((g, p, n, 4), np.uint8)
        nib[..., 0::2] = words & 0xF
        nib[..., 1::2] = words >> 4
        vals = E2M1[nib]
    vals = vals * np.repeat(np.exp2(scales.astype(np.float64) - 127.0), 8, axis=1)[..., None]
    return vals.transpose(0, 1, 3, 2).reshape(g * 512, n)
def pack4(w):
    words, scales = pack_weight(w, "e2m1")
    return words.reshape(words.shape[0], 128, -1), scales


def unpack4(words, scales):
    return unpack_weight(words.reshape(words.shape[0], 128, -1, 2), scales, "e2m1")


def planes(Y):
    n, m = Y.shape
    b = f64(bf(Y)).reshape(n // 32, 32, m)
    amax = np.abs(b).max(1)
    byte = np.clip(np.where(amax > 0, np.frexp(amax)[1] - 1 + 127 - 7, 1), 1, 254)
    codes = (b * np.exp2(127.0 - byte)[:, None, :]).reshape(n, m).astype(np.float32).astype(ml_dtypes.float8_e4m3fn).view(np.uint8)
    words = codes.reshape(n // 512, 128, 4, m).transpose(0, 1, 3, 2)
    return np.ascontiguousarray(words), np.ascontiguousarray(byte.astype(np.uint8).reshape(n // 512, 16, m))


M, P, B = 512, 1024, 2048

def setup_inputs():
    s = mx_kscale(P)
    t = mx_kscale(B)
    a = np.random.randn(P, B) ** 4 / (3.0 * P)
    a = a * np.exp(0.4 * np.random.randn(P, 1)) * np.exp(0.4 * np.random.randn(1, B))
    x = np.exp(0.7 * np.random.randn(1, P) + 0.3 * np.random.randn(M, P))
    measured = np.exp(0.8 * np.random.randn(M, B))
    background = 0.3 * np.exp(0.5 * np.random.randn(B))
    fwd_words, fwd_scales = pack4(a * s[:, None])
    back_words, back_scales = pack4(a.T / t[:, None])
    inv_sens = s / a.sum(axis=1)
    return {"x": bf(x / s), "measured": bf(measured * t),
            "background": bf(background), "inv_sens": bf(inv_sens),
            "fwd_words": fwd_words, "fwd_scales": fwd_scales,
            "back_words": back_words, "back_scales": back_scales}

def reference(x, measured, background, inv_sens, fwd_words, fwd_scales, back_words, back_scales):
    x = f64(x)
    F = unpack4(fwd_words, fwd_scales)
    G = unpack4(back_words, back_scales)
    expected = (mxq(x, 1, "e4m3") @ F) + f64(background)
    ratio = f64(measured) / expected
    back = mxq(ratio, 1, "e4m3") @ G
    y = x * back * f64(inv_sens)
    Y = y.T
    words, scales = planes(Y)
    return y, words, scales

@@ -1,0 +1,513 @@
+from contextlib import ExitStack
+
+import concourse.mybir as mybir
+from concourse.masks import make_identity
+
+M, PIX, BINS = 512, 1024, 2048
+FLOPS = 2 * 2 * M * PIX * BINS
+
+F32 = mybir.dt.float32
+BF16 = mybir.dt.bfloat16
+I32 = mybir.dt.int32
+U32 = mybir.dt.uint32
+U8 = mybir.dt.uint8
+FP8X4 = mybir.dt.float8_e4m3fn_x4
+FP4X4 = mybir.dt.float4_e2m1fn_x4
+ACT = mybir.ActivationFunctionType
+ALU = mybir.AluOpType
+
+P = 128
+K_PASS = 512
+TILES = M // P
+PIX_GROUPS = PIX // K_PASS
+BIN_GROUPS = BINS // K_PASS
+CHUNKS = TILES * BIN_GROUPS
+
+
+def pairs_apart(ap):
+    return ap.rearrange("m (p u e) -> m u p e", u=2, e=2)
+
+
+def as_upe(ap):
+    return ap.rearrange("m (u p e) -> m u p e", u=2, e=2)
+
+
+def tile_mlem_image_update_h1_kernel(
+    tc, x, measured, background, inv_sens, fwd_words, fwd_scales, back_words, back_scales, out_0, out_1, out_2
+):
+    nc = tc.nc
+    V, A, G = nc.vector, nc.scalar, nc.gpsimd
+    with ExitStack() as ctx:
+        keep = ctx.enter_context(tc.tile_pool(name="keep", bufs=1))
+        work = ctx.enter_context(tc.tile_pool(name="work", bufs=8))
+        psum = ctx.enter_context(tc.psum_pool(name="psum", bufs=1))
+        ctx.enter_context(tc.manual_schedule())
+
+        def kept(name, shape, dtype):
+            return keep.tile(shape, dtype, name=name, align_bytes=64)
+
+        ident = kept("ident", [P, P], F32)
+        warm_in = kept("warm_in", [P, 8], F32)
+        warm_out = kept("warm_out", [P, 8], F32)
+        bg_col = kept("bg_col", [P, BIN_GROUPS, 4], BF16)
+        inv_col = kept("inv_col", [P, 8], BF16)
+        bg_sb = [kept("bg_sb%d" % j, [P, 1024], BF16) for j in range(2)]
+        inv_sb = kept("inv_sb", [P, PIX], BF16)
+        x_all = [kept("x_sb%d" % i, [P, PIX], BF16) for i in range(TILES)]
+        x_sb = [[t[:, :K_PASS], t[:, K_PASS:]] for t in x_all]
+        meas = [[kept("meas%d_%d" % (i, j), [P, 1024], BF16) for j in range(2)] for i in range(TILES)]
+        f_words = [kept("f_words%d" % g, [P, PIX_GROUPS, 1024], U8) for g in range(BIN_GROUPS)]
+        f_scales = [kept("f_scales%d" % j, [P, PIX_GROUPS, 1024], U8) for j in range(2)]
+        g_words = [kept("g_words%d" % g, [P, 2 * PIX], U8) for g in range(BIN_GROUPS)]
+        g_scales = [kept("g_scales%d" % j, [P, 2, PIX], U8) for j in range(2)]
+        xs = [[kept("xs%d_%d" % (i, h), [P, K_PASS], F32) for h in range(2)] for i in range(TILES)]
+        x_codes = [kept("x_codes%d" % i, [P, PIX_GROUPS * P], U32) for i in range(TILES)]
+        x_scales = [kept("x_scales%d" % i, [P, PIX_GROUPS * P], U8) for i in range(TILES)]
+        y_codes = kept("y_codes", [P, PIX_GROUPS, M], U32)
+        y_scales = kept("y_scales", [P, PIX_GROUPS, M], U8)
+        live = {}
+
+        def load_x(i):
+            nc.sync.dma_start(out=x_all[i][:], in_=x[P * i : P * (i + 1), :])
+
+        def load_x_half(i, h):
+            nc.sync.dma_start(out=x_sb[i][h], in_=x[P * i : P * (i + 1), K_PASS * h : K_PASS * (h + 1)])
+
+        def load_meas(i, j):
+            nc.sync.dma_start(out=meas[i][j][:], in_=measured[P * i : P * (i + 1), 1024 * j : 1024 * (j + 1)])
+
+        def load_f(g):
+            src = fwd_words[:, :, 1024 * g : 1024 * (g + 1)].rearrange("g p n -> p g n")
+            nc.sync.dma_start(out=f_words[g][:].bitcast(I32), in_=src.bitcast(I32))
+
+        def load_g(g):
+            nc.sync.dma_start(out=g_words[g][:].bitcast(I32), in_=back_words[g].bitcast(I32))
+
+        def load_scales(plane, rows):
+            for q in range(4):
+                src = rows[:, 4 * q : 4 * q + 4, :].rearrange("g r n -> r g n")
+                nc.sync.dma_start(out=plane[32 * q : 32 * q + 4, :, :].bitcast(I32), in_=src.bitcast(I32))
+
+        def move(eng, out, in_):
+            if eng is A:
+                nc.scalar.copy(out=out, in_=in_)
+            else:
+                eng.tensor_copy(out=out, in_=in_)
+
+        def turn_bank():
+            bank = psum.tile([P, 4, P], F32, name="turn", bufs=3)
+            return bank
+
+        def spread(col_words, first, key):
+            bank = turn_bank()
+            for j in range(4):
+                nc.tensor.transpose(bank[:, j, :], col_words[:, first + j : first + j + 1].to_broadcast([P, P]), ident[:])
+            live[key] = bank
+
+        def inv_turn():
+            spread(inv_col[:].bitcast(F32), 0, "inv")
+
+        def inv_copy(eng):
+            move(eng, inv_sb[:].bitcast(F32).rearrange("p (n j) -> p n j", j=4), live["inv"][:].rearrange("p j n -> p n j"))
+
+        def bg_turn(j):
+            spread(bg_col[:].rearrange("p c t -> p (c t)").bitcast(F32), 4 * j, ("bg", j))
+
+        def bg_copy(j, eng):
+            move(eng, bg_sb[j][:].bitcast(F32), live["bg", j][:].rearrange("p j n -> p (j n)"))
+
+        def x_turn(i, hs):
+            bank = turn_bank()
+            for n, h in enumerate(hs):
+                words = x_sb[i][h].bitcast(F32)
+                for u in range(2):
+                    nc.tensor.transpose(bank[:, 2 * n + u, :], words[:, u::2], ident[:])
+            live["xT", i, hs[0]] = bank
+
+        def interleave(bank, groups, name, eng):
+            grouped = work.tile([P, 1024], BF16, name=name, align_bytes=64, bufs=4)
+            move(
+                eng,
+                grouped[:, : K_PASS * groups].bitcast(F32).rearrange("p (g m u) -> p g m u", g=groups, u=2),
+                bank[:, : 2 * groups, :].rearrange("p (g u) m -> p g m u", u=2),
+            )
+            return grouped
+
+        def x_copy(i, hs, eng):
+            live["xg", i, hs[0]] = interleave(live["xT", i, hs[0]], len(hs), "x_grouped", eng)
+
+        def x_quant(i, hs):
+            cols = slice(P * hs[0], P * (hs[-1] + 1))
+            nc.vector.quantize_mx(
+                out=x_codes[i][:, cols].bitcast(FP8X4),
+                scales=x_scales[i][:, cols],
+                in_=live["xg", i, hs[0]][:, : K_PASS * len(hs)],
+            )
+
+        def scale_x(i, h, eng):
+            cols = slice(K_PASS * h, K_PASS * (h + 1))
+            eng.tensor_tensor(out=xs[i][h][:], in0=x_sb[i][h], in1=inv_sb[:, cols], op=ALU.mult)
+
+        def project(c):
+            i, g = divmod(c, BIN_GROUPS)
+            bank = psum.tile([P, K_PASS], F32, name="expected", bufs=3)
+            cols = slice(K_PASS * (g % 2), K_PASS * (g % 2 + 1))
+            for k in range(PIX_GROUPS):
+                nc.tensor.matmul_mx(
+                    out=bank[:],
+                    lhsT=x_codes[i][:, P * k : P * (k + 1)].bitcast(FP8X4),
+                    lhsT_scale=x_scales[i][:, P * k : P * (k + 1)],
+                    rhs=f_words[g][:, k, :].bitcast(FP4X4),
+                    rhs_scale=f_scales[g // 2][:, k, cols],
+                    start=(k == 0),
+                    stop=(k == PIX_GROUPS - 1),
+                )
+            live["e", c] = bank
+
+        def add_bg(c):
+            g = c % BIN_GROUPS
+            cols = slice(K_PASS * (g % 2), K_PASS * (g % 2 + 1))
+            d = work.tile([P, K_PASS], F32, name="denom")
+            nc.vector.tensor_tensor(
+                out=as_upe(d[:]), in0=pairs_apart(live["e", c][:]), in1=as_upe(bg_sb[g // 2][:, cols]), op=ALU.add
+            )
+            live["d", c] = d
+
+        def rsqrt(c):
+            s = work.tile([P, K_PASS], F32, name="root")
+            nc.scalar.activation(out=s[:], in_=live["d", c][:], func=ACT.Abs_reciprocal_sqrt)
+            live["s", c] = s
+
+        def square(c, eng):
+            r = work.tile([P, K_PASS], F32, name="recip")
+            if eng is A:
+                nc.scalar.activation(out=r[:], in_=live["s", c][:], func=ACT.Square)
+            else:
+                eng.tensor_tensor(out=r[:], in0=live["s", c][:], in1=live["s", c][:], op=ALU.mult)
+            live["r", c] = r
+
+        def times_measured(c, eng):
+            i, g = divmod(c, BIN_GROUPS)
+            cols = slice(K_PASS * (g % 2), K_PASS * (g % 2 + 1))
+            ratio = work.tile([P, K_PASS], BF16, name="ratio")
+            eng.tensor_tensor(
+                out=as_upe(ratio[:]), in0=as_upe(live["r", c][:]), in1=pairs_apart(meas[i][g // 2][:, cols]), op=ALU.mult
+            )
+            live["ratio", c] = ratio
+
+        def turn_words(srcs, key):
+            bank = turn_bank()
+            for n, src in enumerate(srcs):
+                words = src[:].bitcast(F32)
+                for u in range(2):
+                    nc.tensor.transpose(bank[:, 2 * n + u, :], words[:, P * u : P * (u + 1)], ident[:])
+            live[key] = bank
+
+        def ratio_turn(cs):
+            turn_words([live["ratio", c] for c in cs], ("rT", cs[0]))
+
+        def ratio_copy(cs, eng):
+            live["rg", cs[0]] = interleave(live["rT", cs[0]], len(cs), "r_grouped", eng)
+
+        def ratio_quant(cs):
+            codes = work.tile([P, 2 * P], U32, name="r_codes", align_bytes=64)
+            scales = work.tile([P, 2 * P], U8, name="r_scales", align_bytes=64)
+            n = len(cs)
+            nc.vector.quantize_mx(
+                out=codes[:, : P * n].bitcast(FP8X4), scales=scales[:, : P * n], in_=live["rg", cs[0]][:, : K_PASS * n]
+            )
+            for a, c in enumerate(cs):
+                live["rq", c] = (codes[:, P * a : P * (a + 1)], scales[:, P * a : P * (a + 1)])
+
+        def back_project(c, h):
+            i, g = divmod(c, BIN_GROUPS)
+            if g == 0:
+                live["b", i, h] = psum.tile([P, K_PASS], F32, name="back%d" % h, bufs=1)
+            codes, scales = live["rq", c]
+            nc.tensor.matmul_mx(
+                out=live["b", i, h][:],
+                lhsT=codes.bitcast(FP8X4),
+                lhsT_scale=scales,
+                rhs=g_words[g][:, 1024 * h : 1024 * (h + 1)].bitcast(FP4X4),
+                rhs_scale=g_scales[g // 2][:, g % 2, K_PASS * h : K_PASS * (h + 1)],
+                start=(g == 0),
+                stop=(g == BIN_GROUPS - 1),
+            )
+
+        def update(i, h):
+            y = work.tile([P, K_PASS], F32, name="y")
+            nc.vector.tensor_tensor(out=y[:], in0=live["b", i, h][:], in1=xs[i][h][:], op=ALU.mult)
+            live["y", i, h] = y
+            nc.sync.dma_start(out=out_0[P * i : P * (i + 1), K_PASS * h : K_PASS * (h + 1)], in_=y[:])
+
+        def y_round(i, h, eng):
+            yb = work.tile([P, K_PASS], BF16, name="y_bf16")
+            if eng is G:
+                eng.tensor_scalar(
+                    out=as_upe(yb[:]), in0=pairs_apart(live["y", i, h][:]), scalar1=1.0, scalar2=0.0, op0=ALU.mult, op1=ALU.add
+                )
+            else:
+                move(eng, as_upe(yb[:]), pairs_apart(live["y", i, h][:]))
+            live["yb", i, h] = yb
+
+        def y_turn(i, hs):
+            turn_words([live["yb", i, h] for h in hs], ("yT", i, hs[0]))
+
+        def y_copy(i, hs, eng):
+            grouped = interleave(live["yT", i, hs[0]], len(hs), "y_grouped", eng)
+            for a, h in enumerate(hs):
+                live["yg", i, h] = grouped[:, K_PASS * a : K_PASS * (a + 1)]
+
+        def y_quant(i, h):
+            cols = slice(P * i, P * (i + 1))
+            nc.vector.quantize_mx(out=y_codes[:, h, cols].bitcast(FP8X4), scales=y_scales[:, h, cols], in_=live["yg", i, h])
+
+        def store_words(i):
+            cols = slice(P * i, P * (i + 1))
+            dst = out_1[:, :, cols, :].rearrange("g p m t -> p g (m t)")
+            nc.sync.dma_start(out=dst.bitcast(I32), in_=y_codes[:, :, cols].bitcast(I32))
+
+        def store_scales():
+            for q in range(4):
+                eng = nc.sync if q % 2 == 0 else nc.scalar
+                dst = out_2[:, 4 * q : 4 * q + 4, :].rearrange("g r m -> r g m")
+                eng.dma_start(out=dst.bitcast(I32), in_=y_scales[32 * q : 32 * q + 4, :, :].bitcast(I32))
+
+        nc.vector.memset(f_scales[0][:].rearrange("p g n -> p (g n)").bitcast(I32), 0)
+        nc.vector.memset(warm_in[:], 1.0)
+        make_identity(nc, ident[:])
+        nc.scalar.activation(out=warm_out[:], in_=warm_in[:], func=ACT.Abs_reciprocal_sqrt)
+        for plane in (f_scales[1], g_scales[0], g_scales[1]):
+            nc.vector.memset(plane[:].rearrange("p g n -> p (g n)").bitcast(I32), 0)
+        nc.sync.dma_start(out=inv_col[:], in_=inv_sens.rearrange("(p t) -> p t", t=8))
+        load_x_half(0, 0)
+        load_x_half(0, 1)
+        nc.sync.dma_start(out=bg_col[:], in_=background.rearrange("(c p t) -> p c t", p=P, t=4))
+        load_scales(f_scales[0], fwd_scales[:, :, 0:1024])
+        load_f(0)
+        load_f(1)
+        load_meas(0, 0)
+        load_scales(f_scales[1], fwd_scales[:, :, 1024:2048])
+        load_f(2)
+        load_x(1)
+        load_f(3)
+        load_meas(0, 1)
+        load_scales(g_scales[0], back_scales[0:2])
+        load_g(0)
+        load_g(1)
+        load_x(2)
+        load_meas(1, 0)
+        load_scales(g_scales[1], back_scales[2:4])
+        load_g(2)
+        load_g(3)
+        load_meas(1, 1)
+        load_x(3)
+        load_meas(2, 0)
+        load_meas(2, 1)
+        load_meas(3, 0)
+        load_meas(3, 1)
+
+        inv_turn()
+        x_turn(0,[0])
+        x_turn(0,[1])
+        x_copy(0,[0], V)
+        inv_copy(A)
+        bg_turn(0)
+        scale_x(0,0, V)
+        x_quant(0,[0])
+        x_copy(0,[1], A)
+        bg_turn(1)
+        x_quant(0,[1])
+        bg_copy(0, V)
+        bg_copy(1, V)
+        project(0)
+        add_bg(0)
+        rsqrt(0)
+        project(1)
+        add_bg(1)
+        rsqrt(1)
+        project(2)
+        x_turn(1,[0, 1])
+        add_bg(2)
+        square(0, A)
+        x_copy(1,[0, 1], V)
+        square(1, A)
+        project(3)
+        add_bg(3)
+        rsqrt(2)
+        rsqrt(3)
+        x_quant(1,[0, 1])
+        project(5)
+        times_measured(1, V)
+        square(2, A)
+        times_measured(0, V)
+        project(4)
+        x_turn(2,[0, 1])
+        ratio_turn([0, 1])
+        add_bg(5)
+        times_measured(2, V)
+        square(3, A)
+        project(7)
+        rsqrt(5)
+        x_copy(2,[0, 1], A)
+        project(6)
+        scale_x(0,1, G)
+        times_measured(3, V)
+        ratio_turn([2, 3])
+        add_bg(4)
+        ratio_copy([0, 1], A)
+        x_quant(2,[0, 1])
+        square(5, A)
+        ratio_quant([0, 1])
+        add_bg(6)
+        rsqrt(4)
+        ratio_copy([2, 3], A)
+        square(4, A)
+        add_bg(7)
+        project(8)
+        rsqrt(7)
+        add_bg(8)
+        back_project(0,1)
+        rsqrt(6)
+        ratio_quant([2, 3])
+        back_project(1,1)
+        rsqrt(8)
+        times_measured(4, V)
+        project(9)
+        square(6, A)
+        project(11)
+        times_measured(5, V)
+        back_project(0,0)
+        add_bg(11)
+        project(10)
+        add_bg(10)
+        square(8, A)
+        x_turn(3,[0, 1])
+        ratio_turn([4, 5])
+        add_bg(9)
+        x_copy(3,[0, 1], A)
+        back_project(1,0)
+        scale_x(1,0, G)
+        square(7, A)
+        times_measured(6, V)
+        back_project(2,1)
+        ratio_copy([4, 5], A)
+        rsqrt(10)
+        x_quant(3,[0, 1])
+        times_measured(8, V)
+        back_project(3,1)
+        times_measured(7, V)
+        back_project(2,0)
+        rsqrt(9)
+        square(10, A)
+        scale_x(1,1, G)
+        ratio_quant([4, 5])
+        back_project(3,0)
+        project(12)
+        rsqrt(11)
+        update(0,1)
+        update(0,0)
+        project(13)
+        project(14)
+        ratio_turn([6, 7])
+        back_project(4,1)
+        back_project(5,1)
+        scale_x(2,0, G)
+        back_project(4,0)
+        scale_x(2,1, G)
+        add_bg(12)
+        ratio_copy([6, 7], A)
+        square(9, A)
+        add_bg(13)
+        back_project(5,0)
+        add_bg(14)
+        ratio_quant([6, 7])
+        rsqrt(13)
+        project(15)
+        back_project(6,1)
+        square(11, A)
+        times_measured(9, V)
+        times_measured(10, V)
+        back_project(6,0)
+        ratio_turn([8, 9])
+        back_project(7,1)
+        times_measured(11, V)
+        square(13, A)
+        rsqrt(12)
+        times_measured(13, V)
+        ratio_copy([8, 9], A)
+        back_project(7,0)
+        square(12, A)
+        update(1,0)
+        ratio_quant([8, 9])
+        rsqrt(14)
+        ratio_turn([10, 11])
+        ratio_copy([10, 11], A)
+        back_project(8,0)
+        times_measured(12, V)
+        add_bg(15)
+        update(1,1)
+        ratio_turn([12, 13])
+        square(14, A)
+        ratio_quant([10, 11])
+        scale_x(3,0, G)
+        back_project(9,0)
+        rsqrt(15)
+        back_project(8,1)
+        times_measured(14, V)
+        y_round(1,1, A)
+        back_project(9,1)
+        back_project(10,0)
+        square(15, A)
+        ratio_copy([12, 13], A)
+        y_round(1,0, V)
+        back_project(10,1)
+        back_project(11,1)
+        y_round(0,0, A)
+        y_round(0,1, V)
+        times_measured(15, V)
+        back_project(11,0)
+        ratio_quant([12, 13])
+        y_turn(1,[0, 1])
+        ratio_turn([14, 15])
+        scale_x(3,1, G)
+        update(2,0)
+        ratio_copy([14, 15], A)
+        update(2,1)
+        y_turn(0,[0, 1])
+        ratio_quant([14, 15])
+        back_project(12,0)
+        back_project(13,0)
+        y_copy(1,[0, 1], A)
+        y_copy(0,[0, 1], A)
+        y_round(2,1, V)
+        back_project(12,1)
+        y_quant(1,1)
+        back_project(13,1)
+        back_project(14,1)
+        y_quant(1,0)
+        store_words(1)
+        back_project(15,1)
+        back_project(14,0)
+        y_quant(0,0)
+        y_round(2,0, A)
+        y_quant(0,1)
+        store_words(0)
+        back_project(15,0)
+        update(3,1)
+        y_turn(2,[0, 1])
+        update(3,0)
+        y_round(3,1, A)
+        y_copy(2,[0, 1], A)
+        y_round(3,0, V)
+        y_turn(3,[1])
+        y_turn(3,[0])
+        y_copy(3,[1], A)
+        y_quant(2,1)
+        y_quant(2,0)
+        store_words(2)
+        y_copy(3,[0], A)
+        y_quant(3,1)
+        y_quant(3,0)
+        store_words(3)
+        store_scales()

@@ -60,12 +60,17 @@ def tile_mlem_image_update_h1_kernel(
         f_scales = [kept("f_scales%d" % j, [P, PIX_GROUPS, 1024], U8) for j in range(2)]
         g_words = [kept("g_words%d" % g, [P, 2 * PIX], U8) for g in range(BIN_GROUPS)]
         g_scales = [kept("g_scales%d" % j, [P, 2, PIX], U8) for j in range(2)]
-        xs = [[kept("xs%d_%d" % (i, h), [P, K_PASS], F32) for h in range(2)] for i in range(TILES)]
         x_codes = [kept("x_codes%d" % i, [P, PIX_GROUPS * P], U32) for i in range(TILES)]
         x_scales = [kept("x_scales%d" % i, [P, PIX_GROUPS * P], U8) for i in range(TILES)]
         y_codes = kept("y_codes", [P, PIX_GROUPS, M], U32)
         y_scales = kept("y_scales", [P, PIX_GROUPS, M], U8)
         live = {}
+        shared = {("x_grouped", (1, 0)): "hand_over0", ("ratio", 2): "hand_over0", ("r_grouped", 0): "hand_over1", ("ratio", 4): "hand_over1", ("r_grouped", 2): "hand_over2", ("ratio", 6): "hand_over2", ("recip", 12): "hand_over3", ("ratio", 15): "hand_over3"}
+
+        def rotating(name, key, shape, dtype, bufs):
+            if (name, key) in shared:
+                return work.tile(shape, dtype, name=name, tag=shared[name, key], bufs=1, align_bytes=64)
+            return work.tile(shape, dtype, name=name, bufs=bufs, align_bytes=64)
 
         def load_x(i):
             nc.sync.dma_start(out=x_all[i][:], in_=x[P * i : P * (i + 1), :])
@@ -124,8 +129,8 @@ def tile_mlem_image_update_h1_kernel(
                     nc.tensor.transpose(bank[:, 2 * n + u, :], words[:, u::2], ident[:])
             live["xT", i, hs[0]] = bank
 
-        def interleave(bank, groups, name, eng):
-            grouped = work.tile([P, 1024], BF16, name=name, align_bytes=64, bufs=4)
+        def interleave(bank, groups, name, key, eng):
+            grouped = rotating(name, key, [P, 1024], BF16, 4)
             move(
                 eng,
                 grouped[:, : K_PASS * groups].bitcast(F32).rearrange("p (g m u) -> p g m u", g=groups, u=2),
@@ -134,7 +139,7 @@ def tile_mlem_image_update_h1_kernel(
             return grouped
 
         def x_copy(i, hs, eng):
-            live["xg", i, hs[0]] = interleave(live["xT", i, hs[0]], len(hs), "x_grouped", eng)
+            live["xg", i, hs[0]] = interleave(live["xT", i, hs[0]], len(hs), "x_grouped", (i, hs[0]), eng)
 
         def x_quant(i, hs):
             cols = slice(P * hs[0], P * (hs[-1] + 1))
@@ -146,7 +151,9 @@ def tile_mlem_image_update_h1_kernel(
 
         def scale_x(i, h, eng):
             cols = slice(K_PASS * h, K_PASS * (h + 1))
-            eng.tensor_tensor(out=xs[i][h][:], in0=x_sb[i][h], in1=inv_sb[:, cols], op=ALU.mult)
+            xs = rotating("xs", (i, h), [P, K_PASS], F32, 8)
+            live["xs", i, h] = xs
+            eng.tensor_tensor(out=xs[:], in0=x_sb[i][h], in1=inv_sb[:, cols], op=ALU.mult)
 
         def project(c):
             i, g = divmod(c, BIN_GROUPS)
@@ -167,19 +174,19 @@ def tile_mlem_image_update_h1_kernel(
         def add_bg(c):
             g = c % BIN_GROUPS
             cols = slice(K_PASS * (g % 2), K_PASS * (g % 2 + 1))
-            d = work.tile([P, K_PASS], F32, name="denom")
+            d = work.tile([P, K_PASS], F32, name="denom", bufs=6)
             nc.vector.tensor_tensor(
                 out=as_upe(d[:]), in0=pairs_apart(live["e", c][:]), in1=as_upe(bg_sb[g // 2][:, cols]), op=ALU.add
             )
             live["d", c] = d
 
         def rsqrt(c):
-            s = work.tile([P, K_PASS], F32, name="root")
+            s = work.tile([P, K_PASS], F32, name="root", bufs=6)
             nc.scalar.activation(out=s[:], in_=live["d", c][:], func=ACT.Abs_reciprocal_sqrt)
             live["s", c] = s
 
         def square(c, eng):
-            r = work.tile([P, K_PASS], F32, name="recip")
+            r = rotating("recip", c, [P, K_PASS], F32, 6)
             if eng is A:
                 nc.scalar.activation(out=r[:], in_=live["s", c][:], func=ACT.Square)
             else:
@@ -189,7 +196,7 @@ def tile_mlem_image_update_h1_kernel(
         def times_measured(c, eng):
             i, g = divmod(c, BIN_GROUPS)
             cols = slice(K_PASS * (g % 2), K_PASS * (g % 2 + 1))
-            ratio = work.tile([P, K_PASS], BF16, name="ratio")
+            ratio = rotating("ratio", c, [P, K_PASS], BF16, 8)
             eng.tensor_tensor(
                 out=as_upe(ratio[:]), in0=as_upe(live["r", c][:]), in1=pairs_apart(meas[i][g // 2][:, cols]), op=ALU.mult
             )
@@ -207,7 +214,7 @@ def tile_mlem_image_update_h1_kernel(
             turn_words([live["ratio", c] for c in cs], ("rT", cs[0]))
 
         def ratio_copy(cs, eng):
-            live["rg", cs[0]] = interleave(live["rT", cs[0]], len(cs), "r_grouped", eng)
+            live["rg", cs[0]] = interleave(live["rT", cs[0]], len(cs), "r_grouped", cs[0], eng)
 
         def ratio_quant(cs):
             codes = work.tile([P, 2 * P], U32, name="r_codes", align_bytes=64)
@@ -236,7 +243,7 @@ def tile_mlem_image_update_h1_kernel(
 
         def update(i, h):
             y = work.tile([P, K_PASS], F32, name="y")
-            nc.vector.tensor_tensor(out=y[:], in0=live["b", i, h][:], in1=xs[i][h][:], op=ALU.mult)
+            nc.vector.tensor_tensor(out=y[:], in0=live["b", i, h][:], in1=live["xs", i, h][:], op=ALU.mult)
             live["y", i, h] = y
             nc.sync.dma_start(out=out_0[P * i : P * (i + 1), K_PASS * h : K_PASS * (h + 1)], in_=y[:])
 
@@ -254,7 +261,7 @@ def tile_mlem_image_update_h1_kernel(
             turn_words([live["yb", i, h] for h in hs], ("yT", i, hs[0]))
 
         def y_copy(i, hs, eng):
-            grouped = interleave(live["yT", i, hs[0]], len(hs), "y_grouped", eng)
+            grouped = interleave(live["yT", i, hs[0]], len(hs), "y_grouped", (i, hs[0]), eng)
             for a, h in enumerate(hs):
                 live["yg", i, h] = grouped[:, K_PASS * a : K_PASS * (a + 1)]
 
@@ -262,10 +269,10 @@ def tile_mlem_image_update_h1_kernel(
             cols = slice(P * i, P * (i + 1))
             nc.vector.quantize_mx(out=y_codes[:, h, cols].bitcast(FP8X4), scales=y_scales[:, h, cols], in_=live["yg", i, h])
 
-        def store_words(i):
+        def store_words(i, h):
             cols = slice(P * i, P * (i + 1))
-            dst = out_1[:, :, cols, :].rearrange("g p m t -> p g (m t)")
-            nc.sync.dma_start(out=dst.bitcast(I32), in_=y_codes[:, :, cols].bitcast(I32))
+            dst = out_1[h, :, cols, :].rearrange("p m t -> p (m t)")
+            nc.sync.dma_start(out=dst.bitcast(I32), in_=y_codes[:, h, cols].bitcast(I32))
 
         def store_scales():
             for q in range(4):
@@ -279,235 +286,238 @@ def tile_mlem_image_update_h1_kernel(
         nc.scalar.activation(out=warm_out[:], in_=warm_in[:], func=ACT.Abs_reciprocal_sqrt)
         for plane in (f_scales[1], g_scales[0], g_scales[1]):
             nc.vector.memset(plane[:].rearrange("p g n -> p (g n)").bitcast(I32), 0)
-        nc.sync.dma_start(out=inv_col[:], in_=inv_sens.rearrange("(p t) -> p t", t=8))
-        load_x_half(0, 0)
-        load_x_half(0, 1)
+        load_x(0)
         nc.sync.dma_start(out=bg_col[:], in_=background.rearrange("(c p t) -> p c t", p=P, t=4))
+        nc.sync.dma_start(out=inv_col[:], in_=inv_sens.rearrange("(p t) -> p t", t=8))
         load_scales(f_scales[0], fwd_scales[:, :, 0:1024])
         load_f(0)
         load_f(1)
-        load_meas(0, 0)
+        load_x(1)
         load_scales(f_scales[1], fwd_scales[:, :, 1024:2048])
         load_f(2)
-        load_x(1)
+        load_meas(0, 0)
         load_f(3)
+        load_x(2)
         load_meas(0, 1)
+        load_x(3)
         load_scales(g_scales[0], back_scales[0:2])
         load_g(0)
         load_g(1)
-        load_x(2)
-        load_meas(1, 0)
         load_scales(g_scales[1], back_scales[2:4])
         load_g(2)
         load_g(3)
+        load_meas(1, 0)
         load_meas(1, 1)
-        load_x(3)
         load_meas(2, 0)
         load_meas(2, 1)
         load_meas(3, 0)
         load_meas(3, 1)
 
-        inv_turn()
         x_turn(0,[0])
         x_turn(0,[1])
         x_copy(0,[0], V)
-        inv_copy(A)
-        bg_turn(0)
-        scale_x(0,0, V)
+        inv_turn()
         x_quant(0,[0])
-        x_copy(0,[1], A)
-        bg_turn(1)
+        x_copy(0,[1], V)
+        bg_turn(0)
+        inv_copy(A)
         x_quant(0,[1])
-        bg_copy(0, V)
-        bg_copy(1, V)
         project(0)
-        add_bg(0)
-        rsqrt(0)
+        bg_copy(0, A)
+        scale_x(0,1, V)
+        scale_x(1,1, G)
         project(1)
-        add_bg(1)
-        rsqrt(1)
-        project(2)
+        add_bg(0)
+        scale_x(1,0, V)
+        rsqrt(0)
+        bg_turn(1)
+        scale_x(0,0, V)
         x_turn(1,[0, 1])
-        add_bg(2)
         square(0, A)
+        add_bg(1)
+        project(2)
+        bg_copy(1, A)
         x_copy(1,[0, 1], V)
+        scale_x(2,0, G)
+        rsqrt(1)
+        x_turn(2,[0, 1])
+        add_bg(2)
         square(1, A)
         project(3)
-        add_bg(3)
-        rsqrt(2)
-        rsqrt(3)
         x_quant(1,[0, 1])
-        project(5)
-        times_measured(1, V)
-        square(2, A)
         times_measured(0, V)
-        project(4)
-        x_turn(2,[0, 1])
-        ratio_turn([0, 1])
-        add_bg(5)
-        times_measured(2, V)
-        square(3, A)
-        project(7)
-        rsqrt(5)
         x_copy(2,[0, 1], A)
-        project(6)
-        scale_x(0,1, G)
-        times_measured(3, V)
-        ratio_turn([2, 3])
+        project(4)
+        add_bg(3)
+        times_measured(1, G)
+        rsqrt(2)
+        project(5)
         add_bg(4)
-        ratio_copy([0, 1], A)
+        rsqrt(3)
+        project(6)
+        add_bg(5)
+        square(2, A)
+        project(7)
         x_quant(2,[0, 1])
-        square(5, A)
-        ratio_quant([0, 1])
-        add_bg(6)
         rsqrt(4)
-        ratio_copy([2, 3], A)
-        square(4, A)
+        add_bg(6)
+        times_measured(2, G)
+        project(9)
+        square(3, A)
         add_bg(7)
-        project(8)
+        ratio_turn([0, 1])
+        rsqrt(5)
+        add_bg(9)
+        times_measured(3, G)
+        x_turn(3,[0, 1])
         rsqrt(7)
+        ratio_copy([0, 1], V)
+        project(11)
+        square(4, A)
+        x_copy(3,[0, 1], V)
+        project(8)
+        rsqrt(9)
+        ratio_quant([0, 1])
+        x_quant(3,[0, 1])
+        square(5, A)
+        add_bg(11)
+        times_measured(4, G)
+        back_project(0,0)
+        project(12)
+        square(7, A)
         add_bg(8)
+        project(15)
+        square(9, A)
+        add_bg(12)
+        times_measured(5, G)
+        project(14)
+        rsqrt(11)
+        add_bg(15)
         back_project(0,1)
         rsqrt(6)
-        ratio_quant([2, 3])
-        back_project(1,1)
-        rsqrt(8)
-        times_measured(4, V)
-        project(9)
-        square(6, A)
-        project(11)
-        times_measured(5, V)
-        back_project(0,0)
-        add_bg(11)
-        project(10)
-        add_bg(10)
-        square(8, A)
-        x_turn(3,[0, 1])
-        ratio_turn([4, 5])
-        add_bg(9)
-        x_copy(3,[0, 1], A)
-        back_project(1,0)
-        scale_x(1,0, G)
-        square(7, A)
-        times_measured(6, V)
-        back_project(2,1)
-        ratio_copy([4, 5], A)
-        rsqrt(10)
-        x_quant(3,[0, 1])
-        times_measured(8, V)
-        back_project(3,1)
-        times_measured(7, V)
-        back_project(2,0)
-        rsqrt(9)
-        square(10, A)
-        scale_x(1,1, G)
-        ratio_quant([4, 5])
-        back_project(3,0)
-        project(12)
-        rsqrt(11)
-        update(0,1)
-        update(0,0)
-        project(13)
-        project(14)
-        ratio_turn([6, 7])
-        back_project(4,1)
-        back_project(5,1)
-        scale_x(2,0, G)
-        back_project(4,0)
-        scale_x(2,1, G)
-        add_bg(12)
-        ratio_copy([6, 7], A)
-        square(9, A)
-        add_bg(13)
-        back_project(5,0)
         add_bg(14)
-        ratio_quant([6, 7])
-        rsqrt(13)
-        project(15)
-        back_project(6,1)
-        square(11, A)
+        ratio_turn([2, 3])
+        rsqrt(8)
+        ratio_turn([4, 5])
+        times_measured(7, V)
+        back_project(1,0)
+        ratio_copy([2, 3], A)
         times_measured(9, V)
-        times_measured(10, V)
-        back_project(6,0)
-        ratio_turn([8, 9])
-        back_project(7,1)
-        times_measured(11, V)
-        square(13, A)
+        project(13)
+        ratio_copy([4, 5], A)
+        scale_x(3,0, V)
+        back_project(1,1)
+        square(6, A)
+        project(10)
+        ratio_quant([2, 3])
+        square(11, A)
+        ratio_quant([4, 5])
+        add_bg(13)
+        times_measured(6, G)
+        back_project(2,1)
+        square(8, A)
+        back_project(3,1)
+        add_bg(10)
+        back_project(2,0)
         rsqrt(12)
+        back_project(3,0)
+        update(0,1)
+        times_measured(8, G)
+        rsqrt(13)
+        ratio_turn([6, 7])
+        update(0,0)
+        back_project(4,1)
+        rsqrt(15)
+        ratio_copy([6, 7], V)
+        back_project(4,0)
+        rsqrt(10)
+        back_project(5,0)
+        times_measured(11, V)
+        ratio_turn([8, 9])
+        square(13, A)
+        ratio_quant([6, 7])
+        back_project(5,1)
+        square(10, A)
         times_measured(13, V)
-        ratio_copy([8, 9], A)
-        back_project(7,0)
+        back_project(6,1)
         square(12, A)
-        update(1,0)
-        ratio_quant([8, 9])
-        rsqrt(14)
+        back_project(6,0)
+        times_measured(10, V)
+        back_project(7,0)
+        ratio_copy([8, 9], A)
+        back_project(7,1)
+        times_measured(12, V)
         ratio_turn([10, 11])
+        square(15, A)
+        ratio_quant([8, 9])
+        ratio_turn([12, 13])
+        update(1,0)
+        rsqrt(14)
+        times_measured(15, G)
+        update(1,1)
         ratio_copy([10, 11], A)
         back_project(8,0)
-        times_measured(12, V)
-        add_bg(15)
-        update(1,1)
-        ratio_turn([12, 13])
-        square(14, A)
-        ratio_quant([10, 11])
-        scale_x(3,0, G)
         back_project(9,0)
-        rsqrt(15)
+        square(14, A)
         back_project(8,1)
-        times_measured(14, V)
-        y_round(1,1, A)
+        ratio_quant([10, 11])
         back_project(9,1)
-        back_project(10,0)
-        square(15, A)
         ratio_copy([12, 13], A)
+        y_round(1,1, V)
+        times_measured(14, V)
+        back_project(10,0)
+        y_round(0,1, A)
+        back_project(11,0)
         y_round(1,0, V)
         back_project(10,1)
-        back_project(11,1)
         y_round(0,0, A)
-        y_round(0,1, V)
-        times_measured(15, V)
-        back_project(11,0)
-        ratio_quant([12, 13])
-        y_turn(1,[0, 1])
         ratio_turn([14, 15])
-        scale_x(3,1, G)
+        ratio_quant([12, 13])
         update(2,0)
+        y_turn(1,[0, 1])
         ratio_copy([14, 15], A)
-        update(2,1)
         y_turn(0,[0, 1])
+        scale_x(2,1, V)
+        back_project(11,1)
+        y_copy(1,[0, 1], A)
         ratio_quant([14, 15])
         back_project(12,0)
-        back_project(13,0)
-        y_copy(1,[0, 1], A)
         y_copy(0,[0, 1], A)
-        y_round(2,1, V)
-        back_project(12,1)
-        y_quant(1,1)
-        back_project(13,1)
-        back_project(14,1)
-        y_quant(1,0)
-        store_words(1)
-        back_project(15,1)
+        update(2,1)
+        back_project(13,0)
         back_project(14,0)
-        y_quant(0,0)
         y_round(2,0, A)
-        y_quant(0,1)
-        store_words(0)
+        y_quant(1,1)
+        store_words(1, 1)
         back_project(15,0)
-        update(3,1)
-        y_turn(2,[0, 1])
+        scale_x(3,1, V)
+        back_project(12,1)
+        y_round(2,1, A)
+        back_project(13,1)
+        y_quant(0,1)
+        store_words(0, 1)
         update(3,0)
-        y_round(3,1, A)
+        back_project(14,1)
+        back_project(15,1)
+        y_quant(0,0)
+        store_words(0, 0)
+        y_turn(2,[0, 1])
+        y_round(3,0, A)
+        update(3,1)
         y_copy(2,[0, 1], A)
-        y_round(3,0, V)
-        y_turn(3,[1])
+        y_quant(1,0)
+        store_words(1, 0)
         y_turn(3,[0])
-        y_copy(3,[1], A)
-        y_quant(2,1)
-        y_quant(2,0)
-        store_words(2)
+        y_round(3,1, V)
         y_copy(3,[0], A)
-        y_quant(3,1)
+        y_quant(2,1)
+        store_words(2, 1)
+        y_turn(3,[1])
+        y_quant(2,0)
+        store_words(2, 0)
         y_quant(3,0)
-        store_words(3)
+        store_words(3, 0)
+        y_copy(3,[1], A)
+        y_quant(3,1)
+        store_words(3, 1)
         store_scales()

@@ -25,11 +25,15 @@ CHUNKS = TILES * BIN_GROUPS
 
 
 def pairs_apart(ap):
-    return ap.rearrange("m (p u e) -> m u p e", u=2, e=2)
+    return ap.rearrange("m (q u e) -> m u q e", u=2, e=2)
 
 
-def as_upe(ap):
-    return ap.rearrange("m (u p e) -> m u p e", u=2, e=2)
+def as_uqe(ap):
+    return ap.rearrange("m (u q e) -> m u q e", u=2, e=2)
+
+
+def group_of(ap, groups, a):
+    return ap.rearrange("m (u a p e) -> m a u p e", u=2, a=groups, e=2)[:, a, :, :, :]
 
 
 def tile_mlem_image_update_h1_kernel(
@@ -62,10 +66,15 @@ def tile_mlem_image_update_h1_kernel(
         g_scales = [kept("g_scales%d" % j, [P, 2, PIX], U8) for j in range(2)]
         x_codes = [kept("x_codes%d" % i, [P, PIX_GROUPS * P], U32) for i in range(TILES)]
         x_scales = [kept("x_scales%d" % i, [P, PIX_GROUPS * P], U8) for i in range(TILES)]
+        y_sb = [kept("y_sb%d" % i, [P, PIX], F32) for i in range(TILES)]
         y_codes = kept("y_codes", [P, PIX_GROUPS, M], U32)
         y_scales = kept("y_scales", [P, PIX_GROUPS, M], U8)
         live = {}
-        shared = {("x_grouped", (1, 0)): "hand_over0", ("ratio", 2): "hand_over0", ("r_grouped", 0): "hand_over1", ("ratio", 4): "hand_over1", ("r_grouped", 2): "hand_over2", ("ratio", 6): "hand_over2", ("recip", 12): "hand_over3", ("ratio", 15): "hand_over3"}
+        shared = {("x_grouped", (2, 0)): "hand_over0", ("ratio", 2): "hand_over0"}
+        wide = [1, 2, 4, 3, 5, 6]
+
+        def scalar_group(c):
+            return [c - c % 2, c - c % 2 + 1] if c // 2 in wide else [c]
 
         def rotating(name, key, shape, dtype, bufs):
             if (name, key) in shared:
@@ -103,20 +112,20 @@ def tile_mlem_image_update_h1_kernel(
             bank = psum.tile([P, 4, P], F32, name="turn", bufs=3)
             return bank
 
-        def spread(col_words, first, key):
+        def spread(col_words, picks, key):
             bank = turn_bank()
-            for j in range(4):
-                nc.tensor.transpose(bank[:, j, :], col_words[:, first + j : first + j + 1].to_broadcast([P, P]), ident[:])
+            for j, w in enumerate(picks):
+                nc.tensor.transpose(bank[:, j, :], col_words[:, w : w + 1].to_broadcast([P, P]), ident[:])
             live[key] = bank
 
         def inv_turn():
-            spread(inv_col[:].bitcast(F32), 0, "inv")
+            spread(inv_col[:].bitcast(F32), range(4), "inv")
 
         def inv_copy(eng):
             move(eng, inv_sb[:].bitcast(F32).rearrange("p (n j) -> p n j", j=4), live["inv"][:].rearrange("p j n -> p n j"))
 
         def bg_turn(j):
-            spread(bg_col[:].rearrange("p c t -> p (c t)").bitcast(F32), 4 * j, ("bg", j))
+            spread(bg_col[:].rearrange("p c t -> p (c t)").bitcast(F32), [4 * j + 2 * a + u for u in range(2) for a in range(2)], ("bg", j))
 
         def bg_copy(j, eng):
             move(eng, bg_sb[j][:].bitcast(F32), live["bg", j][:].rearrange("p j n -> p (j n)"))
@@ -149,11 +158,12 @@ def tile_mlem_image_update_h1_kernel(
                 in_=live["xg", i, hs[0]][:, : K_PASS * len(hs)],
             )
 
-        def scale_x(i, h, eng):
-            cols = slice(K_PASS * h, K_PASS * (h + 1))
-            xs = rotating("xs", (i, h), [P, K_PASS], F32, 8)
-            live["xs", i, h] = xs
-            eng.tensor_tensor(out=xs[:], in0=x_sb[i][h], in1=inv_sb[:, cols], op=ALU.mult)
+        def scale_x(i, hs, eng):
+            cols = slice(K_PASS * hs[0], K_PASS * (hs[-1] + 1))
+            xs = rotating("xs", (i, hs[0]), [P, K_PASS * len(hs)], F32, 8)
+            eng.tensor_tensor(out=xs[:], in0=x_all[i][:, cols], in1=inv_sb[:, cols], op=ALU.mult)
+            for a, h in enumerate(hs):
+                live["xs", i, h] = xs[:, K_PASS * a : K_PASS * (a + 1)]
 
         def project(c):
             i, g = divmod(c, BIN_GROUPS)
@@ -173,41 +183,48 @@ def tile_mlem_image_update_h1_kernel(
 
         def add_bg(c):
             g = c % BIN_GROUPS
-            cols = slice(K_PASS * (g % 2), K_PASS * (g % 2 + 1))
-            d = work.tile([P, K_PASS], F32, name="denom", bufs=6)
+            cs = scalar_group(c)
+            if ("d", cs[0]) not in live:
+                live["d", cs[0]] = work.tile([P, K_PASS * len(cs)], F32, name="denom", bufs=4)
             nc.vector.tensor_tensor(
-                out=as_upe(d[:]), in0=pairs_apart(live["e", c][:]), in1=as_upe(bg_sb[g // 2][:, cols]), op=ALU.add
+                out=group_of(live["d", cs[0]][:], len(cs), c - cs[0]),
+                in0=pairs_apart(live["e", c][:]),
+                in1=group_of(bg_sb[g // 2][:], 2, g % 2),
+                op=ALU.add,
             )
-            live["d", c] = d
 
-        def rsqrt(c):
-            s = work.tile([P, K_PASS], F32, name="root", bufs=6)
-            nc.scalar.activation(out=s[:], in_=live["d", c][:], func=ACT.Abs_reciprocal_sqrt)
-            live["s", c] = s
+        def rsqrt(cs):
+            s = work.tile([P, K_PASS * len(cs)], F32, name="root", bufs=4)
+            nc.scalar.activation(out=s[:], in_=live["d", cs[0]][:], func=ACT.Abs_reciprocal_sqrt)
+            live["s", cs[0]] = s
 
-        def square(c, eng):
-            r = rotating("recip", c, [P, K_PASS], F32, 6)
+        def square(cs, eng):
+            r = rotating("recip", cs[0], [P, K_PASS * len(cs)], F32, 4)
+            s = live["s", cs[0]]
             if eng is A:
-                nc.scalar.activation(out=r[:], in_=live["s", c][:], func=ACT.Square)
+                nc.scalar.activation(out=r[:], in_=s[:], func=ACT.Square)
             else:
-                eng.tensor_tensor(out=r[:], in0=live["s", c][:], in1=live["s", c][:], op=ALU.mult)
-            live["r", c] = r
+                eng.tensor_tensor(out=r[:], in0=s[:], in1=s[:], op=ALU.mult)
+            live["r", cs[0]] = r
 
-        def times_measured(c, eng):
-            i, g = divmod(c, BIN_GROUPS)
-            cols = slice(K_PASS * (g % 2), K_PASS * (g % 2 + 1))
-            ratio = rotating("ratio", c, [P, K_PASS], BF16, 8)
-            eng.tensor_tensor(
-                out=as_upe(ratio[:]), in0=as_upe(live["r", c][:]), in1=pairs_apart(meas[i][g // 2][:, cols]), op=ALU.mult
-            )
-            live["ratio", c] = ratio
+        def times_measured(cs, eng):
+            i, g = divmod(cs[0], BIN_GROUPS)
+            cols = slice(K_PASS * (g % 2), K_PASS * (g % 2 + len(cs)))
+            ratio = rotating("ratio", cs[0], [P, K_PASS * len(cs)], BF16, 6)
+            made = scalar_group(cs[0])
+            r = live["r", made[0]]
+            recip = as_uqe(r[:]) if made == cs else group_of(r[:], 2, cs[0] - made[0])
+            eng.tensor_tensor(out=as_uqe(ratio[:]), in0=recip, in1=pairs_apart(meas[i][g // 2][:, cols]), op=ALU.mult)
+            for a, c in enumerate(cs):
+                live["ratio", c] = (ratio, len(cs), a)
 
         def turn_words(srcs, key):
             bank = turn_bank()
-            for n, src in enumerate(srcs):
+            for n, (src, groups, a) in enumerate(srcs):
                 words = src[:].bitcast(F32)
                 for u in range(2):
-                    nc.tensor.transpose(bank[:, 2 * n + u, :], words[:, P * u : P * (u + 1)], ident[:])
+                    first = P * (groups * u + a)
+                    nc.tensor.transpose(bank[:, 2 * n + u, :], words[:, first : first + P], ident[:])
             live[key] = bank
 
         def ratio_turn(cs):
@@ -242,20 +259,16 @@ def tile_mlem_image_update_h1_kernel(
             )
 
         def update(i, h):
-            y = work.tile([P, K_PASS], F32, name="y")
-            nc.vector.tensor_tensor(out=y[:], in0=live["b", i, h][:], in1=live["xs", i, h][:], op=ALU.mult)
-            live["y", i, h] = y
-            nc.sync.dma_start(out=out_0[P * i : P * (i + 1), K_PASS * h : K_PASS * (h + 1)], in_=y[:])
+            cols = slice(K_PASS * h, K_PASS * (h + 1))
+            nc.vector.tensor_tensor(out=y_sb[i][:, cols], in0=live["b", i, h][:], in1=live["xs", i, h], op=ALU.mult)
+            nc.sync.dma_start(out=out_0[P * i : P * (i + 1), cols], in_=y_sb[i][:, cols])
 
-        def y_round(i, h, eng):
-            yb = work.tile([P, K_PASS], BF16, name="y_bf16")
-            if eng is G:
-                eng.tensor_scalar(
-                    out=as_upe(yb[:]), in0=pairs_apart(live["y", i, h][:]), scalar1=1.0, scalar2=0.0, op0=ALU.mult, op1=ALU.add
-                )
-            else:
-                move(eng, as_upe(yb[:]), pairs_apart(live["y", i, h][:]))
-            live["yb", i, h] = yb
+        def y_round(i, hs, eng):
+            cols = slice(K_PASS * hs[0], K_PASS * (hs[-1] + 1))
+            yb = work.tile([P, K_PASS * len(hs)], BF16, name="y_bf16", bufs=5)
+            move(eng, as_uqe(yb[:]), pairs_apart(y_sb[i][:, cols]))
+            for a, h in enumerate(hs):
+                live["yb", i, h] = (yb, len(hs), a)
 
         def y_turn(i, hs):
             turn_words([live["yb", i, h] for h in hs], ("yT", i, hs[0]))
@@ -313,211 +326,193 @@ def tile_mlem_image_update_h1_kernel(
         load_meas(3, 0)
         load_meas(3, 1)
 
-        x_turn(0,[0])
         x_turn(0,[1])
-        x_copy(0,[0], V)
-        inv_turn()
-        x_quant(0,[0])
+        x_turn(0,[0])
         x_copy(0,[1], V)
-        bg_turn(0)
-        inv_copy(A)
+        inv_turn()
+        x_copy(0,[0], A)
         x_quant(0,[1])
-        project(0)
-        bg_copy(0, A)
-        scale_x(0,1, V)
-        scale_x(1,1, G)
+        bg_turn(0)
+        x_quant(0,[0])
+        inv_copy(A)
         project(1)
-        add_bg(0)
-        scale_x(1,0, V)
-        rsqrt(0)
-        bg_turn(1)
-        scale_x(0,0, V)
-        x_turn(1,[0, 1])
-        square(0, A)
+        bg_copy(0, A)
+        scale_x(0,[1], V)
+        scale_x(1,[1], G)
+        project(0)
         add_bg(1)
-        project(2)
+        scale_x(0,[0], G)
+        rsqrt([1])
+        bg_turn(1)
+        add_bg(0)
+        x_turn(1,[0, 1])
+        scale_x(1,[0], G)
         bg_copy(1, A)
+        project(2)
         x_copy(1,[0, 1], V)
-        scale_x(2,0, G)
-        rsqrt(1)
-        x_turn(2,[0, 1])
-        add_bg(2)
-        square(1, A)
+        rsqrt([0])
+        scale_x(2,[0], G)
         project(3)
-        x_quant(1,[0, 1])
-        times_measured(0, V)
-        x_copy(2,[0, 1], A)
-        project(4)
+        add_bg(2)
+        square([1], A)
+        x_turn(2,[0, 1])
         add_bg(3)
-        times_measured(1, G)
-        rsqrt(2)
+        square([0], A)
+        x_turn(3,[0, 1])
+        x_quant(1,[0, 1])
+        rsqrt([2, 3])
+        x_copy(2,[0, 1], V)
+        times_measured([0], G)
+        project(4)
+        x_copy(3,[0, 1], V)
+        times_measured([1], G)
         project(5)
+        square([2, 3], A)
         add_bg(4)
-        rsqrt(3)
         project(6)
         add_bg(5)
-        square(2, A)
         project(7)
         x_quant(2,[0, 1])
-        rsqrt(4)
-        add_bg(6)
-        times_measured(2, G)
-        project(9)
-        square(3, A)
-        add_bg(7)
+        rsqrt([4, 5])
         ratio_turn([0, 1])
-        rsqrt(5)
-        add_bg(9)
-        times_measured(3, G)
-        x_turn(3,[0, 1])
-        rsqrt(7)
-        ratio_copy([0, 1], V)
-        project(11)
-        square(4, A)
-        x_copy(3,[0, 1], V)
-        project(8)
-        rsqrt(9)
-        ratio_quant([0, 1])
         x_quant(3,[0, 1])
-        square(5, A)
-        add_bg(11)
-        times_measured(4, G)
-        back_project(0,0)
-        project(12)
-        square(7, A)
+        times_measured([2], G)
+        add_bg(6)
+        project(8)
+        add_bg(7)
+        ratio_copy([0, 1], A)
+        project(9)
+        times_measured([3], G)
         add_bg(8)
-        project(15)
-        square(9, A)
-        add_bg(12)
-        times_measured(5, G)
-        project(14)
-        rsqrt(11)
-        add_bg(15)
-        back_project(0,1)
-        rsqrt(6)
-        add_bg(14)
-        ratio_turn([2, 3])
-        rsqrt(8)
-        ratio_turn([4, 5])
-        times_measured(7, V)
-        back_project(1,0)
-        ratio_copy([2, 3], A)
-        times_measured(9, V)
-        project(13)
-        ratio_copy([4, 5], A)
-        scale_x(3,0, V)
-        back_project(1,1)
-        square(6, A)
+        square([4, 5], A)
         project(10)
-        ratio_quant([2, 3])
-        square(11, A)
-        ratio_quant([4, 5])
-        add_bg(13)
-        times_measured(6, G)
-        back_project(2,1)
-        square(8, A)
-        back_project(3,1)
+        add_bg(9)
+        project(11)
+        ratio_quant([0, 1])
+        project(12)
+        rsqrt([8, 9])
+        times_measured([4, 5], V)
+        back_project(0,0)
+        back_project(1,0)
+        back_project(0,1)
+        rsqrt([6, 7])
         add_bg(10)
+        back_project(1,1)
+        square([8, 9], G)
+        ratio_turn([2, 3])
+        add_bg(11)
+        ratio_turn([4, 5])
+        ratio_copy([2, 3], A)
+        project(14)
+        add_bg(12)
+        square([6, 7], A)
+        ratio_copy([4, 5], V)
+        project(13)
+        ratio_quant([2, 3])
+        project(15)
+        ratio_quant([4, 5])
+        rsqrt([10, 11])
+        times_measured([8, 9], V)
+        back_project(2,1)
+        back_project(3,1)
         back_project(2,0)
-        rsqrt(12)
         back_project(3,0)
-        update(0,1)
-        times_measured(8, G)
-        rsqrt(13)
-        ratio_turn([6, 7])
-        update(0,0)
-        back_project(4,1)
-        rsqrt(15)
-        ratio_copy([6, 7], V)
-        back_project(4,0)
-        rsqrt(10)
-        back_project(5,0)
-        times_measured(11, V)
+        add_bg(13)
+        times_measured([6], G)
+        square([10, 11], A)
         ratio_turn([8, 9])
-        square(13, A)
-        ratio_quant([6, 7])
-        back_project(5,1)
-        square(10, A)
-        times_measured(13, V)
-        back_project(6,1)
-        square(12, A)
-        back_project(6,0)
-        times_measured(10, V)
-        back_project(7,0)
+        add_bg(14)
+        times_measured([7], V)
+        rsqrt([12, 13])
+        times_measured([11], G)
+        update(0,0)
+        ratio_turn([6, 7])
+        update(0,1)
         ratio_copy([8, 9], A)
-        back_project(7,1)
-        times_measured(12, V)
+        back_project(4,0)
+        times_measured([10], G)
+        back_project(5,0)
+        ratio_copy([6, 7], V)
+        square([12, 13], A)
+        back_project(4,1)
+        back_project(5,1)
+        add_bg(15)
         ratio_turn([10, 11])
-        square(15, A)
+        ratio_quant([6, 7])
+        rsqrt([15])
         ratio_quant([8, 9])
-        ratio_turn([12, 13])
-        update(1,0)
-        rsqrt(14)
-        times_measured(15, G)
-        update(1,1)
+        times_measured([12, 13], V)
+        back_project(6,0)
+        square([15], A)
+        back_project(7,0)
+        back_project(6,1)
         ratio_copy([10, 11], A)
+        back_project(7,1)
+        update(1,0)
+        times_measured([15], G)
+        ratio_turn([12, 13])
+        rsqrt([14])
+        update(1,1)
         back_project(8,0)
-        back_project(9,0)
-        square(14, A)
-        back_project(8,1)
         ratio_quant([10, 11])
+        back_project(9,0)
+        square([14], A)
+        back_project(8,1)
+        scale_x(2,[1], V)
         back_project(9,1)
         ratio_copy([12, 13], A)
-        y_round(1,1, V)
-        times_measured(14, V)
-        back_project(10,0)
-        y_round(0,1, A)
-        back_project(11,0)
-        y_round(1,0, V)
         back_project(10,1)
-        y_round(0,0, A)
+        times_measured([14], V)
+        back_project(10,0)
+        y_round(1,[0, 1], A)
+        back_project(11,1)
+        y_round(0,[0, 1], V)
+        back_project(11,0)
         ratio_turn([14, 15])
         ratio_quant([12, 13])
-        update(2,0)
-        y_turn(1,[0, 1])
-        ratio_copy([14, 15], A)
         y_turn(0,[0, 1])
-        scale_x(2,1, V)
-        back_project(11,1)
-        y_copy(1,[0, 1], A)
-        ratio_quant([14, 15])
-        back_project(12,0)
-        y_copy(0,[0, 1], A)
+        update(2,0)
+        ratio_copy([14, 15], A)
+        y_turn(1,[0, 1])
         update(2,1)
+        y_copy(0,[0, 1], A)
+        back_project(12,0)
+        ratio_quant([14, 15])
         back_project(13,0)
-        back_project(14,0)
-        y_round(2,0, A)
-        y_quant(1,1)
-        store_words(1, 1)
-        back_project(15,0)
-        scale_x(3,1, V)
+        y_copy(1,[0, 1], A)
         back_project(12,1)
-        y_round(2,1, A)
+        scale_x(3,[0], V)
         back_project(13,1)
+        back_project(14,0)
+        y_round(2,[0, 1], A)
         y_quant(0,1)
         store_words(0, 1)
-        update(3,0)
+        scale_x(3,[1], V)
+        back_project(15,0)
         back_project(14,1)
         back_project(15,1)
-        y_quant(0,0)
-        store_words(0, 0)
+        update(3,0)
         y_turn(2,[0, 1])
-        y_round(3,0, A)
         update(3,1)
-        y_copy(2,[0, 1], A)
+        y_round(3,[0], A)
         y_quant(1,0)
         store_words(1, 0)
+        y_quant(0,0)
+        store_words(0, 0)
+        y_copy(2,[0, 1], A)
+        y_round(3,[1], V)
         y_turn(3,[0])
-        y_round(3,1, V)
+        y_quant(1,1)
+        store_words(1, 1)
         y_copy(3,[0], A)
+        y_turn(3,[1])
         y_quant(2,1)
         store_words(2, 1)
-        y_turn(3,[1])
         y_quant(2,0)
         store_words(2, 0)
+        y_copy(3,[1], A)
         y_quant(3,0)
         store_words(3, 0)
-        y_copy(3,[1], A)
         y_quant(3,1)
         store_words(3, 1)
         store_scales()

@@ -21,7 +21,6 @@ K_PASS = 512
 TILES = M // P
 PIX_GROUPS = PIX // K_PASS
 BIN_GROUPS = BINS // K_PASS
-CHUNKS = TILES * BIN_GROUPS
 
 
 def pairs_apart(ap):
@@ -32,10 +31,6 @@ def as_uqe(ap):
     return ap.rearrange("m (u q e) -> m u q e", u=2, e=2)
 
 
-def group_of(ap, groups, a):
-    return ap.rearrange("m (u a p e) -> m a u p e", u=2, a=groups, e=2)[:, a, :, :, :]
-
-
 def tile_mlem_image_update_h1_kernel(
     tc, x, measured, background, inv_sens, fwd_words, fwd_scales, back_words, back_scales, out_0, out_1, out_2
 ):
@@ -43,56 +38,57 @@ def tile_mlem_image_update_h1_kernel(
     V, A, G = nc.vector, nc.scalar, nc.gpsimd
     with ExitStack() as ctx:
         keep = ctx.enter_context(tc.tile_pool(name="keep", bufs=1))
-        work = ctx.enter_context(tc.tile_pool(name="work", bufs=8))
+        work = ctx.enter_context(tc.tile_pool(name="work", bufs=4))
         psum = ctx.enter_context(tc.psum_pool(name="psum", bufs=1))
         ctx.enter_context(tc.manual_schedule())
 
+        live = {}
+        shared = {"xs3_0": "f_raw_words2", "xs1_0": "ratio0_2", "xs0_0": "ratio1_2", "xs1_1": "ratio3_0", "xs2_0": "ratio2_2"}
+        back_banks = [["back0", "back1"], ["back2", "back3"], ["back0", "back1"], ["back2", "back3"]]
+
         def kept(name, shape, dtype):
-            return keep.tile(shape, dtype, name=name, align_bytes=64)
+            return keep.tile(shape, dtype, name=name, tag=shared.get(name, name), align_bytes=64)
 
         ident = kept("ident", [P, P], F32)
         warm_in = kept("warm_in", [P, 8], F32)
         warm_out = kept("warm_out", [P, 8], F32)
         bg_col = kept("bg_col", [P, BIN_GROUPS, 4], BF16)
         inv_col = kept("inv_col", [P, 8], BF16)
-        bg_sb = [kept("bg_sb%d" % j, [P, 1024], BF16) for j in range(2)]
         inv_sb = kept("inv_sb", [P, PIX], BF16)
-        x_all = [kept("x_sb%d" % i, [P, PIX], BF16) for i in range(TILES)]
-        x_sb = [[t[:, :K_PASS], t[:, K_PASS:]] for t in x_all]
+        x_sb = [kept("x_sb%d" % i, [P, PIX], BF16) for i in range(TILES)]
         meas = [[kept("meas%d_%d" % (i, j), [P, 1024], BF16) for j in range(2)] for i in range(TILES)]
-        f_words = [kept("f_words%d" % g, [P, PIX_GROUPS, 1024], U8) for g in range(BIN_GROUPS)]
-        f_scales = [kept("f_scales%d" % j, [P, PIX_GROUPS, 1024], U8) for j in range(2)]
+        f_raw_words = [kept("f_raw_words%d" % g, [P, PIX_GROUPS, 1024], U8) for g in range(BIN_GROUPS)]
+        f_raw_scales = [kept("f_raw_scales%d" % j, [P, PIX_GROUPS, n * K_PASS], U8) for j, n in enumerate((1, 3))]
+        f_words = [kept("f_words%d" % g, [P, 2, PIX_GROUPS, 2, 2 * P], U8) for g in range(BIN_GROUPS)]
+        f_scales = [kept("f_scales%d" % g, [P, 2, PIX_GROUPS, 2, P], U8) for g in range(BIN_GROUPS)]
         g_words = [kept("g_words%d" % g, [P, 2 * PIX], U8) for g in range(BIN_GROUPS)]
         g_scales = [kept("g_scales%d" % j, [P, 2, PIX], U8) for j in range(2)]
-        x_codes = [kept("x_codes%d" % i, [P, PIX_GROUPS * P], U32) for i in range(TILES)]
-        x_scales = [kept("x_scales%d" % i, [P, PIX_GROUPS * P], U8) for i in range(TILES)]
+        x_codes = kept("x_codes", [P, PIX_GROUPS, M], U32)
+        x_scales = kept("x_scales", [P, PIX_GROUPS, M], U8)
+        roots = [kept("roots%d" % g, [P, 4, M], F32) for g in range(BIN_GROUPS)]
+        recips = [kept("recips%d" % g, [P, 2, M, 2], F32) for g in range(BIN_GROUPS)]
+        r_codes = [kept("r_codes%d" % g, [P, M], U32) for g in range(BIN_GROUPS)]
+        r_scales = [kept("r_scales%d" % g, [P, M], U8) for g in range(BIN_GROUPS)]
         y_sb = [kept("y_sb%d" % i, [P, PIX], F32) for i in range(TILES)]
         y_codes = kept("y_codes", [P, PIX_GROUPS, M], U32)
         y_scales = kept("y_scales", [P, PIX_GROUPS, M], U8)
-        live = {}
-        shared = {("x_grouped", (2, 0)): "hand_over0", ("ratio", 2): "hand_over0"}
-        wide = [1, 2, 4, 3, 5, 6]
 
-        def scalar_group(c):
-            return [c - c % 2, c - c % 2 + 1] if c // 2 in wide else [c]
-
-        def rotating(name, key, shape, dtype, bufs):
-            if (name, key) in shared:
-                return work.tile(shape, dtype, name=name, tag=shared[name, key], bufs=1, align_bytes=64)
-            return work.tile(shape, dtype, name=name, bufs=bufs, align_bytes=64)
+        def images(first, count):
+            return slice(P * first, P * (first + count))
 
         def load_x(i):
-            nc.sync.dma_start(out=x_all[i][:], in_=x[P * i : P * (i + 1), :])
+            nc.sync.dma_start(out=x_sb[i][:], in_=x[images(i, 1), :])
 
-        def load_x_half(i, h):
-            nc.sync.dma_start(out=x_sb[i][h], in_=x[P * i : P * (i + 1), K_PASS * h : K_PASS * (h + 1)])
+        def load_x_half(i, k):
+            cols = slice(K_PASS * k, K_PASS * (k + 1))
+            nc.sync.dma_start(out=x_sb[i][:, cols], in_=x[images(i, 1), cols])
 
         def load_meas(i, j):
-            nc.sync.dma_start(out=meas[i][j][:], in_=measured[P * i : P * (i + 1), 1024 * j : 1024 * (j + 1)])
+            nc.sync.dma_start(out=meas[i][j][:], in_=measured[images(i, 1), 1024 * j : 1024 * (j + 1)])
 
         def load_f(g):
             src = fwd_words[:, :, 1024 * g : 1024 * (g + 1)].rearrange("g p n -> p g n")
-            nc.sync.dma_start(out=f_words[g][:].bitcast(I32), in_=src.bitcast(I32))
+            nc.sync.dma_start(out=f_raw_words[g][:].bitcast(I32), in_=src.bitcast(I32))
 
         def load_g(g):
             nc.sync.dma_start(out=g_words[g][:].bitcast(I32), in_=back_words[g].bitcast(I32))
@@ -108,150 +104,145 @@ def tile_mlem_image_update_h1_kernel(
             else:
                 eng.tensor_copy(out=out, in_=in_)
 
-        def turn_bank():
-            bank = psum.tile([P, 4, P], F32, name="turn", bufs=3)
-            return bank
-
-        def spread(col_words, picks, key):
-            bank = turn_bank()
-            for j, w in enumerate(picks):
-                nc.tensor.transpose(bank[:, j, :], col_words[:, w : w + 1].to_broadcast([P, P]), ident[:])
-            live[key] = bank
+        def bank(role, shape):
+            bufs = {"turn": 2, "expected": 2}.get(role, 1)
+            return psum.tile(shape, F32, name=role, tag=role, bufs=bufs)
 
         def inv_turn():
-            spread(inv_col[:].bitcast(F32), range(4), "inv")
+            turned = bank("turn", [P, 4, P])
+            words = inv_col[:].bitcast(F32)
+            for j in range(4):
+                nc.tensor.transpose(turned[:, j, :], words[:, j : j + 1].to_broadcast([P, P]), ident[:])
+            live["inv"] = turned
 
         def inv_copy(eng):
             move(eng, inv_sb[:].bitcast(F32).rearrange("p (n j) -> p n j", j=4), live["inv"][:].rearrange("p j n -> p n j"))
 
-        def bg_turn(j):
-            spread(bg_col[:].rearrange("p c t -> p (c t)").bitcast(F32), [4 * j + 2 * a + u for u in range(2) for a in range(2)], ("bg", j))
-
-        def bg_copy(j, eng):
-            move(eng, bg_sb[j][:].bitcast(F32), live["bg", j][:].rearrange("p j n -> p (j n)"))
-
-        def x_turn(i, hs):
-            bank = turn_bank()
-            for n, h in enumerate(hs):
-                words = x_sb[i][h].bitcast(F32)
+        def x_turn(i, ks):
+            turned = bank("back%d" % i if ks[0] == 0 else "turn", [P, 4, P])
+            words = x_sb[i][:].bitcast(F32)
+            for n, k in enumerate(ks):
                 for u in range(2):
-                    nc.tensor.transpose(bank[:, 2 * n + u, :], words[:, u::2], ident[:])
-            live["xT", i, hs[0]] = bank
+                    nc.tensor.transpose(turned[:, 2 * n + u, :], words[:, 2 * P * k + u : 2 * P * (k + 1) : 2], ident[:])
+            live["xT", i, ks[0]] = turned
 
-        def interleave(bank, groups, name, key, eng):
-            grouped = rotating(name, key, [P, 1024], BF16, 4)
+        def interleave(turned, groups, name, eng):
+            grouped = work.tile([P, 1024], BF16, name=name, bufs=5, align_bytes=64)
             move(
                 eng,
                 grouped[:, : K_PASS * groups].bitcast(F32).rearrange("p (g m u) -> p g m u", g=groups, u=2),
-                bank[:, : 2 * groups, :].rearrange("p (g u) m -> p g m u", u=2),
+                turned[:, : 2 * groups, :].rearrange("p (g u) m -> p g m u", u=2),
             )
             return grouped
 
-        def x_copy(i, hs, eng):
-            live["xg", i, hs[0]] = interleave(live["xT", i, hs[0]], len(hs), "x_grouped", (i, hs[0]), eng)
+        def x_copy(i, ks, eng):
+            grouped = interleave(live["xT", i, ks[0]], len(ks), "x_grouped", eng)
+            for n, k in enumerate(ks):
+                live["xg", i, k] = grouped[:, K_PASS * n : K_PASS * (n + 1)]
 
-        def x_quant(i, hs):
-            cols = slice(P * hs[0], P * (hs[-1] + 1))
+        def x_quant(i, k):
             nc.vector.quantize_mx(
-                out=x_codes[i][:, cols].bitcast(FP8X4),
-                scales=x_scales[i][:, cols],
-                in_=live["xg", i, hs[0]][:, : K_PASS * len(hs)],
+                out=x_codes[:, k, images(i, 1)].bitcast(FP8X4),
+                scales=x_scales[:, k, images(i, 1)],
+                in_=live["xg", i, k],
             )
 
         def scale_x(i, hs, eng):
             cols = slice(K_PASS * hs[0], K_PASS * (hs[-1] + 1))
-            xs = rotating("xs", (i, hs[0]), [P, K_PASS * len(hs)], F32, 8)
-            eng.tensor_tensor(out=xs[:], in0=x_all[i][:, cols], in1=inv_sb[:, cols], op=ALU.mult)
+            xs = kept("xs%d_%d" % (i, hs[0]), [P, K_PASS * len(hs)], F32)
+            eng.tensor_tensor(out=xs[:], in0=x_sb[i][:, cols], in1=inv_sb[:, cols], op=ALU.mult)
             for a, h in enumerate(hs):
                 live["xs", i, h] = xs[:, K_PASS * a : K_PASS * (a + 1)]
 
-        def project(c):
-            i, g = divmod(c, BIN_GROUPS)
-            bank = psum.tile([P, K_PASS], F32, name="expected", bufs=3)
-            cols = slice(K_PASS * (g % 2), K_PASS * (g % 2 + 1))
-            for k in range(PIX_GROUPS):
-                nc.tensor.matmul_mx(
-                    out=bank[:],
-                    lhsT=x_codes[i][:, P * k : P * (k + 1)].bitcast(FP8X4),
-                    lhsT_scale=x_scales[i][:, P * k : P * (k + 1)],
-                    rhs=f_words[g][:, k, :].bitcast(FP4X4),
-                    rhs_scale=f_scales[g // 2][:, k, cols],
-                    start=(k == 0),
-                    stop=(k == PIX_GROUPS - 1),
+        def sort_words(g, u):
+            nc.vector.tensor_copy(
+                out=f_words[g][:, u, :, :, :].rearrange("p k e (n b) -> p k e n b", b=2),
+                in_=f_raw_words[g][:].rearrange("p k (n u e b) -> p u k e n b", u=2, e=2, b=2)[:, u, :, :, :, :],
+            )
+
+        def sort_scales(g, us):
+            raw = f_raw_scales[min(g, 1)][:, :, K_PASS * max(g - 1, 0) : K_PASS * max(g, 1)]
+            picked = slice(us[0], us[-1] + 1)
+            nc.vector.tensor_copy(
+                out=f_scales[g][:, picked, :, :, :],
+                in_=raw.rearrange("p k (n u e) -> p u k e n", u=2, e=2)[:, picked, :, :, :],
+            )
+
+        def project(g, first, count, j, part=None):
+            slots = 4 // count
+            part = part or range(slots)
+            if part[0] == 0:
+                live["e", g, first, j] = bank("expected", [P, slots, P * count])
+            expected = live["e", g, first, j]
+            runs = [(first, count)] if count == TILES else [(i, 1) for i in range(first, first + count)]
+            for s in part:
+                u, e = divmod(slots * j + s, 2)
+                for i, n in runs:
+                    for k in range(PIX_GROUPS):
+                        nc.tensor.matmul_mx(
+                            out=expected[:, s, images(i - first, n)],
+                            lhsT=f_words[g][:, u, k, e, :].bitcast(FP4X4),
+                            lhsT_scale=f_scales[g][:, u, k, e, :],
+                            rhs=x_codes[:, k, images(i, n)].bitcast(FP8X4),
+                            rhs_scale=x_scales[:, k, images(i, n)],
+                            start=(k == 0),
+                            stop=(k == PIX_GROUPS - 1),
+                        )
+
+        def rsqrt(g, first, count, j):
+            slots = 4 // count
+            for s in range(slots):
+                t = slots * j + s
+                nc.scalar.activation(
+                    out=roots[g][:, t, images(first, count)],
+                    in_=live["e", g, first, j][:, s, :],
+                    func=ACT.Abs_reciprocal_sqrt,
+                    bias=bg_col[:, g, t : t + 1],
                 )
-            live["e", c] = bank
 
-        def add_bg(c):
-            g = c % BIN_GROUPS
-            cs = scalar_group(c)
-            if ("d", cs[0]) not in live:
-                live["d", cs[0]] = work.tile([P, K_PASS * len(cs)], F32, name="denom", bufs=4)
-            nc.vector.tensor_tensor(
-                out=group_of(live["d", cs[0]][:], len(cs), c - cs[0]),
-                in0=pairs_apart(live["e", c][:]),
-                in1=group_of(bg_sb[g // 2][:], 2, g % 2),
-                op=ALU.add,
-            )
-
-        def rsqrt(cs):
-            s = work.tile([P, K_PASS * len(cs)], F32, name="root", bufs=4)
-            nc.scalar.activation(out=s[:], in_=live["d", cs[0]][:], func=ACT.Abs_reciprocal_sqrt)
-            live["s", cs[0]] = s
-
-        def square(cs, eng):
-            r = rotating("recip", cs[0], [P, K_PASS * len(cs)], F32, 4)
-            s = live["s", cs[0]]
+        def square(g, first, count, us, eng):
+            picked = slice(us[0], us[-1] + 1)
+            src = roots[g][:, :, images(first, count)].rearrange("p (u e) m -> p u m e", e=2)[:, picked, :, :]
+            dst = recips[g][:, picked, images(first, count), :]
             if eng is A:
-                nc.scalar.activation(out=r[:], in_=s[:], func=ACT.Square)
+                nc.scalar.activation(out=dst, in_=src, func=ACT.Square)
             else:
-                eng.tensor_tensor(out=r[:], in0=s[:], in1=s[:], op=ALU.mult)
-            live["r", cs[0]] = r
+                eng.tensor_tensor(out=dst, in0=src, in1=src, op=ALU.mult)
 
-        def times_measured(cs, eng):
-            i, g = divmod(cs[0], BIN_GROUPS)
-            cols = slice(K_PASS * (g % 2), K_PASS * (g % 2 + len(cs)))
-            ratio = rotating("ratio", cs[0], [P, K_PASS * len(cs)], BF16, 6)
-            made = scalar_group(cs[0])
-            r = live["r", made[0]]
-            recip = as_uqe(r[:]) if made == cs else group_of(r[:], 2, cs[0] - made[0])
-            eng.tensor_tensor(out=as_uqe(ratio[:]), in0=recip, in1=pairs_apart(meas[i][g // 2][:, cols]), op=ALU.mult)
-            for a, c in enumerate(cs):
-                live["ratio", c] = (ratio, len(cs), a)
-
-        def turn_words(srcs, key):
-            bank = turn_bank()
-            for n, (src, groups, a) in enumerate(srcs):
-                words = src[:].bitcast(F32)
+        def meas_turn(g, half):
+            turned = bank("turn", [P, 2, 2 * P])
+            for a in range(2):
+                words = meas[2 * half + a][g // 2][:].bitcast(F32)
                 for u in range(2):
-                    first = P * (groups * u + a)
-                    nc.tensor.transpose(bank[:, 2 * n + u, :], words[:, first : first + P], ident[:])
-            live[key] = bank
+                    start = 2 * P * (g % 2)
+                    nc.tensor.transpose(turned[:, u, images(a, 1)], words[:, start + u : start + 2 * P : 2], ident[:])
+            live["mT", g, half] = turned
 
-        def ratio_turn(cs):
-            turn_words([live["ratio", c] for c in cs], ("rT", cs[0]))
-
-        def ratio_copy(cs, eng):
-            live["rg", cs[0]] = interleave(live["rT", cs[0]], len(cs), "r_grouped", cs[0], eng)
-
-        def ratio_quant(cs):
-            codes = work.tile([P, 2 * P], U32, name="r_codes", align_bytes=64)
-            scales = work.tile([P, 2 * P], U8, name="r_scales", align_bytes=64)
-            n = len(cs)
-            nc.vector.quantize_mx(
-                out=codes[:, : P * n].bitcast(FP8X4), scales=scales[:, : P * n], in_=live["rg", cs[0]][:, : K_PASS * n]
+        def times_measured(g, first, count):
+            ratio = kept("ratio%d_%d" % (g, first), [P, K_PASS * count], BF16)
+            turned = live["mT", g, first // 2][:].bitcast(BF16).rearrange("p u (m e) -> p m u e", e=2)
+            nc.vector.tensor_tensor(
+                out=ratio[:].rearrange("p (m u e) -> p m u e", u=2, e=2),
+                in0=recips[g][:, :, images(first, count), :].rearrange("p u m e -> p m u e"),
+                in1=turned[:, images(first % 2, count), :, :],
+                op=ALU.mult,
             )
-            for a, c in enumerate(cs):
-                live["rq", c] = (codes[:, P * a : P * (a + 1)], scales[:, P * a : P * (a + 1)])
+            live["ratio", g, first] = ratio
 
-        def back_project(c, h):
-            i, g = divmod(c, BIN_GROUPS)
+        def ratio_quant(g, first, count):
+            nc.vector.quantize_mx(
+                out=r_codes[g][:, images(first, count)].bitcast(FP8X4),
+                scales=r_scales[g][:, images(first, count)],
+                in_=live["ratio", g, first][:],
+            )
+
+        def back_project(i, g, h):
             if g == 0:
-                live["b", i, h] = psum.tile([P, K_PASS], F32, name="back%d" % h, bufs=1)
-            codes, scales = live["rq", c]
+                live["b", i, h] = bank(back_banks[i][h], [P, K_PASS])
             nc.tensor.matmul_mx(
                 out=live["b", i, h][:],
-                lhsT=codes.bitcast(FP8X4),
-                lhsT_scale=scales,
+                lhsT=r_codes[g][:, images(i, 1)].bitcast(FP8X4),
+                lhsT_scale=r_scales[g][:, images(i, 1)],
                 rhs=g_words[g][:, 1024 * h : 1024 * (h + 1)].bitcast(FP4X4),
                 rhs_scale=g_scales[g // 2][:, g % 2, K_PASS * h : K_PASS * (h + 1)],
                 start=(g == 0),
@@ -261,31 +252,43 @@ def tile_mlem_image_update_h1_kernel(
         def update(i, h):
             cols = slice(K_PASS * h, K_PASS * (h + 1))
             nc.vector.tensor_tensor(out=y_sb[i][:, cols], in0=live["b", i, h][:], in1=live["xs", i, h], op=ALU.mult)
-            nc.sync.dma_start(out=out_0[P * i : P * (i + 1), cols], in_=y_sb[i][:, cols])
+            nc.sync.dma_start(out=out_0[images(i, 1), cols], in_=y_sb[i][:, cols])
 
         def y_round(i, hs, eng):
-            cols = slice(K_PASS * hs[0], K_PASS * (hs[-1] + 1))
-            yb = work.tile([P, K_PASS * len(hs)], BF16, name="y_bf16", bufs=5)
-            move(eng, as_uqe(yb[:]), pairs_apart(y_sb[i][:, cols]))
-            for a, h in enumerate(hs):
-                live["yb", i, h] = (yb, len(hs), a)
+            for h in hs:
+                yb = work.tile([P, K_PASS], BF16, name="y_bf16", bufs=8)
+                move(eng, as_uqe(yb[:]), pairs_apart(y_sb[i][:, K_PASS * h : K_PASS * (h + 1)]))
+                live["yb", i, h] = yb
+
+        def y_direct(i, h):
+            yb = work.tile([P, K_PASS], BF16, name="y_bf16", bufs=8)
+            nc.vector.tensor_tensor(
+                out=as_uqe(yb[:]), in0=pairs_apart(live["b", i, h][:]), in1=pairs_apart(live["xs", i, h]), op=ALU.mult
+            )
+            live["yb", i, h] = yb
 
         def y_turn(i, hs):
-            turn_words([live["yb", i, h] for h in hs], ("yT", i, hs[0]))
+            turned = bank("turn", [P, 4, P])
+            for n, h in enumerate(hs):
+                words = live["yb", i, h][:].bitcast(F32)
+                for u in range(2):
+                    nc.tensor.transpose(turned[:, 2 * n + u, :], words[:, P * u : P * (u + 1)], ident[:])
+            live["yT", i, hs[0]] = turned
 
         def y_copy(i, hs, eng):
-            grouped = interleave(live["yT", i, hs[0]], len(hs), "y_grouped", (i, hs[0]), eng)
+            grouped = interleave(live["yT", i, hs[0]], len(hs), "y_grouped", eng)
             for a, h in enumerate(hs):
                 live["yg", i, h] = grouped[:, K_PASS * a : K_PASS * (a + 1)]
 
         def y_quant(i, h):
-            cols = slice(P * i, P * (i + 1))
-            nc.vector.quantize_mx(out=y_codes[:, h, cols].bitcast(FP8X4), scales=y_scales[:, h, cols], in_=live["yg", i, h])
+            nc.vector.quantize_mx(
+                out=y_codes[:, h, images(i, 1)].bitcast(FP8X4), scales=y_scales[:, h, images(i, 1)], in_=live["yg", i, h]
+            )
 
-        def store_words(i, h):
-            cols = slice(P * i, P * (i + 1))
-            dst = out_1[h, :, cols, :].rearrange("p m t -> p (m t)")
-            nc.sync.dma_start(out=dst.bitcast(I32), in_=y_codes[:, h, cols].bitcast(I32))
+        def store_words(i, hs):
+            picked = slice(hs[0], hs[-1] + 1)
+            dst = out_1[picked, :, images(i, 1), :].rearrange("g p m t -> p g (m t)")
+            nc.sync.dma_start(out=dst.bitcast(I32), in_=y_codes[:, picked, images(i, 1)].bitcast(I32))
 
         def store_scales():
             for q in range(4):
@@ -293,226 +296,231 @@ def tile_mlem_image_update_h1_kernel(
                 dst = out_2[:, 4 * q : 4 * q + 4, :].rearrange("g r m -> r g m")
                 eng.dma_start(out=dst.bitcast(I32), in_=y_scales[32 * q : 32 * q + 4, :, :].bitcast(I32))
 
-        nc.vector.memset(f_scales[0][:].rearrange("p g n -> p (g n)").bitcast(I32), 0)
+        def clear(eng, plane):
+            eng.memset(plane[:].rearrange("p g n -> p (g n)").bitcast(I32), 0)
+
+        clear(V, f_raw_scales[0])
         nc.vector.memset(warm_in[:], 1.0)
         make_identity(nc, ident[:])
         nc.scalar.activation(out=warm_out[:], in_=warm_in[:], func=ACT.Abs_reciprocal_sqrt)
-        for plane in (f_scales[1], g_scales[0], g_scales[1]):
-            nc.vector.memset(plane[:].rearrange("p g n -> p (g n)").bitcast(I32), 0)
-        load_x(0)
-        nc.sync.dma_start(out=bg_col[:], in_=background.rearrange("(c p t) -> p c t", p=P, t=4))
-        nc.sync.dma_start(out=inv_col[:], in_=inv_sens.rearrange("(p t) -> p t", t=8))
-        load_scales(f_scales[0], fwd_scales[:, :, 0:1024])
+        clear(V, f_raw_scales[1])
+        clear(V, g_scales[0])
+        clear(V, g_scales[1])
+        load_x_half(0, 0)
+        load_x_half(0, 1)
         load_f(0)
-        load_f(1)
         load_x(1)
-        load_scales(f_scales[1], fwd_scales[:, :, 1024:2048])
-        load_f(2)
-        load_meas(0, 0)
-        load_f(3)
+        load_scales(f_raw_scales[0], fwd_scales[:, :, :K_PASS])
+        nc.sync.dma_start(out=bg_col[:], in_=background.rearrange("(c p t) -> p c t", p=P, t=4))
         load_x(2)
-        load_meas(0, 1)
         load_x(3)
+        load_scales(f_raw_scales[1], fwd_scales[:, :, K_PASS:])
+        load_f(1)
+        load_meas(0, 0)
+        load_meas(1, 0)
+        nc.sync.dma_start(out=inv_col[:], in_=inv_sens.rearrange("(p t) -> p t", t=8))
+        load_meas(2, 0)
+        load_meas(3, 0)
         load_scales(g_scales[0], back_scales[0:2])
         load_g(0)
+        load_f(2)
         load_g(1)
+        load_meas(0, 1)
+        load_meas(1, 1)
+        load_f(3)
+        load_meas(2, 1)
+        load_meas(3, 1)
         load_scales(g_scales[1], back_scales[2:4])
         load_g(2)
         load_g(3)
-        load_meas(1, 0)
-        load_meas(1, 1)
-        load_meas(2, 0)
-        load_meas(2, 1)
-        load_meas(3, 0)
-        load_meas(3, 1)
 
-        x_turn(0,[1])
-        x_turn(0,[0])
-        x_copy(0,[1], V)
+        x_turn(0, [0])
+        x_turn(0, [1])
+        x_copy(0, [0], A)
+        sort_words(0, 0)
+        x_copy(0, [1], A)
+        x_turn(1, [0, 1])
+        x_quant(0, 0)
+        x_quant(0, 1)
+        sort_scales(0, [0])
+        sort_scales(0, [1])
+        x_turn(2, [0, 1])
+        x_copy(1, [0, 1], A)
+        sort_words(0, 1)
+        x_quant(1, 0)
+        x_quant(1, 1)
+        project(0, 0, 1, 0, [0, 1])
+        x_copy(2, [0, 1], A)
+        sort_scales(1, [0, 1])
+        project(0, 0, 1, 0, [2, 3])
+        x_quant(2, 0)
+        x_quant(2, 1)
+        project(0, 1, 1, 0)
+        sort_words(1, 0)
+        rsqrt(0, 0, 1, 0)
+        sort_words(1, 1)
+        x_turn(3, [0, 1])
+        square(0, 0, 1, [0, 1], A)
+        sort_scales(3, [0, 1])
+        project(0, 2, 1, 0)
+        rsqrt(0, 1, 1, 0)
+        x_copy(3, [0, 1], V)
+        meas_turn(0, 0)
+        square(0, 1, 1, [0, 1], A)
         inv_turn()
-        x_copy(0,[0], A)
-        x_quant(0,[1])
-        bg_turn(0)
-        x_quant(0,[0])
-        inv_copy(A)
-        project(1)
-        bg_copy(0, A)
-        scale_x(0,[1], V)
-        scale_x(1,[1], G)
-        project(0)
-        add_bg(1)
-        scale_x(0,[0], G)
-        rsqrt([1])
-        bg_turn(1)
-        add_bg(0)
-        x_turn(1,[0, 1])
-        scale_x(1,[0], G)
-        bg_copy(1, A)
-        project(2)
-        x_copy(1,[0, 1], V)
-        rsqrt([0])
-        scale_x(2,[0], G)
-        project(3)
-        add_bg(2)
-        square([1], A)
-        x_turn(2,[0, 1])
-        add_bg(3)
-        square([0], A)
-        x_turn(3,[0, 1])
-        x_quant(1,[0, 1])
-        rsqrt([2, 3])
-        x_copy(2,[0, 1], V)
-        times_measured([0], G)
-        project(4)
-        x_copy(3,[0, 1], V)
-        times_measured([1], G)
-        project(5)
-        square([2, 3], A)
-        add_bg(4)
-        project(6)
-        add_bg(5)
-        project(7)
-        x_quant(2,[0, 1])
-        rsqrt([4, 5])
-        ratio_turn([0, 1])
-        x_quant(3,[0, 1])
-        times_measured([2], G)
-        add_bg(6)
-        project(8)
-        add_bg(7)
-        ratio_copy([0, 1], A)
-        project(9)
-        times_measured([3], G)
-        add_bg(8)
-        square([4, 5], A)
-        project(10)
-        add_bg(9)
-        project(11)
-        ratio_quant([0, 1])
-        project(12)
-        rsqrt([8, 9])
-        times_measured([4, 5], V)
-        back_project(0,0)
-        back_project(1,0)
-        back_project(0,1)
-        rsqrt([6, 7])
-        add_bg(10)
-        back_project(1,1)
-        square([8, 9], G)
-        ratio_turn([2, 3])
-        add_bg(11)
-        ratio_turn([4, 5])
-        ratio_copy([2, 3], A)
-        project(14)
-        add_bg(12)
-        square([6, 7], A)
-        ratio_copy([4, 5], V)
-        project(13)
-        ratio_quant([2, 3])
-        project(15)
-        ratio_quant([4, 5])
-        rsqrt([10, 11])
-        times_measured([8, 9], V)
-        back_project(2,1)
-        back_project(3,1)
-        back_project(2,0)
-        back_project(3,0)
-        add_bg(13)
-        times_measured([6], G)
-        square([10, 11], A)
-        ratio_turn([8, 9])
-        add_bg(14)
-        times_measured([7], V)
-        rsqrt([12, 13])
-        times_measured([11], G)
-        update(0,0)
-        ratio_turn([6, 7])
-        update(0,1)
-        ratio_copy([8, 9], A)
-        back_project(4,0)
-        times_measured([10], G)
-        back_project(5,0)
-        ratio_copy([6, 7], V)
-        square([12, 13], A)
-        back_project(4,1)
-        back_project(5,1)
-        add_bg(15)
-        ratio_turn([10, 11])
-        ratio_quant([6, 7])
-        rsqrt([15])
-        ratio_quant([8, 9])
-        times_measured([12, 13], V)
-        back_project(6,0)
-        square([15], A)
-        back_project(7,0)
-        back_project(6,1)
-        ratio_copy([10, 11], A)
-        back_project(7,1)
-        update(1,0)
-        times_measured([15], G)
-        ratio_turn([12, 13])
-        rsqrt([14])
-        update(1,1)
-        back_project(8,0)
-        ratio_quant([10, 11])
-        back_project(9,0)
-        square([14], A)
-        back_project(8,1)
-        scale_x(2,[1], V)
-        back_project(9,1)
-        ratio_copy([12, 13], A)
-        back_project(10,1)
-        times_measured([14], V)
-        back_project(10,0)
-        y_round(1,[0, 1], A)
-        back_project(11,1)
-        y_round(0,[0, 1], V)
-        back_project(11,0)
-        ratio_turn([14, 15])
-        ratio_quant([12, 13])
-        y_turn(0,[0, 1])
-        update(2,0)
-        ratio_copy([14, 15], A)
-        y_turn(1,[0, 1])
-        update(2,1)
-        y_copy(0,[0, 1], A)
-        back_project(12,0)
-        ratio_quant([14, 15])
-        back_project(13,0)
-        y_copy(1,[0, 1], A)
-        back_project(12,1)
-        scale_x(3,[0], V)
-        back_project(13,1)
-        back_project(14,0)
-        y_round(2,[0, 1], A)
-        y_quant(0,1)
-        store_words(0, 1)
-        scale_x(3,[1], V)
-        back_project(15,0)
-        back_project(14,1)
-        back_project(15,1)
-        update(3,0)
-        y_turn(2,[0, 1])
-        update(3,1)
-        y_round(3,[0], A)
-        y_quant(1,0)
-        store_words(1, 0)
-        y_quant(0,0)
-        store_words(0, 0)
-        y_copy(2,[0, 1], A)
-        y_round(3,[1], V)
-        y_turn(3,[0])
-        y_quant(1,1)
-        store_words(1, 1)
-        y_copy(3,[0], A)
-        y_turn(3,[1])
-        y_quant(2,1)
-        store_words(2, 1)
-        y_quant(2,0)
-        store_words(2, 0)
-        y_copy(3,[1], A)
-        y_quant(3,0)
-        store_words(3, 0)
-        y_quant(3,1)
-        store_words(3, 1)
+        x_quant(3, 0)
+        rsqrt(0, 2, 1, 0)
+        x_quant(3, 1)
+        times_measured(0, 0, 1)
+        project(0, 3, 1, 0)
+        square(0, 2, 1, [0, 1], A)
+        times_measured(0, 1, 1)
+        project(1, 0, 4, 1)
+        ratio_quant(0, 0, 1)
+        rsqrt(0, 3, 1, 0)
+        sort_scales(2, [0, 1])
+        meas_turn(0, 1)
+        rsqrt(1, 0, 4, 1)
+        ratio_quant(0, 1, 1)
+        sort_words(2, 0)
+        project(1, 0, 4, 0)
+        square(0, 3, 1, [0, 1], A)
+        inv_copy(V)
+        project(1, 0, 4, 2)
+        rsqrt(1, 0, 4, 0)
+        sort_words(2, 1)
+        back_project(0, 0, 1)
+        rsqrt(1, 0, 4, 2)
+        back_project(0, 0, 0)
+        back_project(1, 0, 1)
+        times_measured(0, 2, 1)
+        scale_x(3, [0], G)
+        project(1, 0, 4, 3)
+        square(1, 0, 4, [0], A)
+        times_measured(0, 3, 1)
+        project(2, 0, 2, 1)
+        rsqrt(1, 0, 4, 3)
+        ratio_quant(0, 3, 1)
+        meas_turn(1, 1)
+        sort_words(3, 0)
+        rsqrt(2, 0, 2, 1)
+        meas_turn(1, 0)
+        sort_words(3, 1)
+        square(1, 0, 4, [1], A)
+        project(2, 0, 2, 0)
+        scale_x(3, [1], V)
+        project(3, 0, 2, 0)
+        ratio_quant(0, 2, 1)
+        rsqrt(2, 0, 2, 0)
+        scale_x(1, [0], G)
+        times_measured(1, 2, 2)
+        back_project(1, 0, 0)
+        rsqrt(3, 0, 2, 0)
+        project(3, 0, 2, 1)
+        square(2, 0, 2, [0], A)
+        times_measured(1, 0, 2)
+        scale_x(2, [1], G)
+        project(2, 2, 2, 1)
+        rsqrt(3, 0, 2, 1)
+        meas_turn(2, 0)
+        square(2, 0, 2, [1], A)
+        ratio_quant(1, 0, 2)
+        meas_turn(3, 0)
+        ratio_quant(1, 2, 2)
+        square(3, 0, 2, [1], A)
+        project(2, 2, 2, 0)
+        times_measured(2, 0, 2)
+        scale_x(0, [0], G)
+        square(3, 0, 2, [0], A)
+        back_project(1, 1, 0)
+        rsqrt(2, 2, 2, 1)
+        back_project(0, 1, 1)
+        times_measured(3, 0, 2)
+        back_project(1, 1, 1)
+        back_project(0, 1, 0)
+        rsqrt(2, 2, 2, 0)
+        project(3, 2, 1, 0)
+        square(2, 2, 2, [1], A)
+        ratio_quant(2, 0, 2)
+        meas_turn(2, 1)
+        scale_x(0, [1], V)
+        square(2, 2, 2, [0], A)
+        ratio_quant(3, 0, 2)
+        meas_turn(3, 1)
+        rsqrt(3, 2, 1, 0)
+        scale_x(1, [1], G)
+        times_measured(2, 2, 2)
+        back_project(0, 2, 1)
+        back_project(0, 3, 1)
+        square(3, 2, 1, [0, 1], A)
+        project(3, 3, 1, 0)
+        update(0, 1)
+        back_project(0, 2, 0)
+        rsqrt(3, 3, 1, 0)
+        back_project(0, 3, 0)
+        ratio_quant(2, 2, 2)
+        back_project(1, 2, 1)
+        scale_x(2, [0], G)
+        update(0, 0)
+        back_project(1, 2, 0)
+        y_round(0, [1], A)
+        back_project(1, 3, 0)
+        times_measured(3, 2, 1)
+        back_project(2, 0, 1)
+        y_round(0, [0], A)
+        back_project(1, 3, 1)
+        update(1, 0)
+        back_project(2, 1, 1)
+        square(3, 3, 1, [0, 1], A)
+        back_project(2, 0, 0)
+        ratio_quant(3, 2, 1)
+        back_project(2, 2, 1)
+        update(1, 1)
+        y_round(1, [0], A)
+        back_project(2, 1, 0)
+        back_project(3, 0, 0)
+        times_measured(3, 3, 1)
+        back_project(2, 3, 1)
+        y_round(1, [1], A)
+        back_project(2, 2, 0)
+        update(2, 1)
+        back_project(2, 3, 0)
+        y_turn(0, [0, 1])
+        ratio_quant(3, 3, 1)
+        update(2, 0)
+        y_turn(1, [0, 1])
+        y_copy(0, [0, 1], A)
+        back_project(3, 1, 0)
+        y_round(2, [1], V)
+        back_project(3, 2, 0)
+        y_copy(1, [0, 1], A)
+        y_quant(0, 0)
+        back_project(3, 3, 0)
+        back_project(3, 0, 1)
+        y_round(2, [0], A)
+        update(3, 0)
+        back_project(3, 1, 1)
+        back_project(3, 2, 1)
+        y_quant(1, 0)
+        back_project(3, 3, 1)
+        y_quant(1, 1)
+        store_words(1, [0, 1])
+        y_round(3, [0], A)
+        y_quant(0, 1)
+        store_words(0, [0, 1])
+        y_turn(2, [0, 1])
+        y_direct(3, 1)
+        y_copy(2, [0, 1], A)
+        update(3, 1)
+        y_turn(3, [1])
+        y_copy(3, [1], A)
+        y_turn(3, [0])
+        y_quant(2, 0)
+        y_quant(2, 1)
+        store_words(2, [0, 1])
+        y_copy(3, [0], A)
+        y_quant(3, 1)
+        store_words(3, [1])
+        y_quant(3, 0)
+        store_words(3, [0])
         store_scales()

from contextlib import ExitStack

import concourse.mybir as mybir
from concourse.masks import make_identity

M, PIX, BINS = 512, 1024, 2048
FLOPS = 2 * 2 * M * PIX * BINS

F32 = mybir.dt.float32
BF16 = mybir.dt.bfloat16
I32 = mybir.dt.int32
U32 = mybir.dt.uint32
U8 = mybir.dt.uint8
FP8X4 = mybir.dt.float8_e4m3fn_x4
FP4X4 = mybir.dt.float4_e2m1fn_x4
ACT = mybir.ActivationFunctionType
ALU = mybir.AluOpType

P = 128
K_PASS = 512
TILES = M // P
PIX_GROUPS = PIX // K_PASS
BIN_GROUPS = BINS // K_PASS


def pairs_apart(ap):
    return ap.rearrange("m (q u e) -> m u q e", u=2, e=2)


def as_uqe(ap):
    return ap.rearrange("m (u q e) -> m u q e", u=2, e=2)


def tile_mlem_image_update_h1_kernel(
    tc, x, measured, background, inv_sens, fwd_words, fwd_scales, back_words, back_scales, out_0, out_1, out_2
):
    nc = tc.nc
    V, A, G = nc.vector, nc.scalar, nc.gpsimd
    with ExitStack() as ctx:
        keep = ctx.enter_context(tc.tile_pool(name="keep", bufs=1))
        work = ctx.enter_context(tc.tile_pool(name="work", bufs=4))
        psum = ctx.enter_context(tc.psum_pool(name="psum", bufs=1))
        ctx.enter_context(tc.manual_schedule())

        live = {}
        shared = {"xs3_0": "f_raw_words2", "xs1_0": "ratio0_2", "xs0_0": "ratio1_2", "xs1_1": "ratio3_0", "xs2_0": "ratio2_2"}
        back_banks = [["back0", "back1"], ["back2", "back3"], ["back0", "back1"], ["back2", "back3"]]

        def kept(name, shape, dtype):
            return keep.tile(shape, dtype, name=name, tag=shared.get(name, name), align_bytes=64)

        ident = kept("ident", [P, P], F32)
        warm_in = kept("warm_in", [P, 8], F32)
        warm_out = kept("warm_out", [P, 8], F32)
        bg_col = kept("bg_col", [P, BIN_GROUPS, 4], BF16)
        inv_col = kept("inv_col", [P, 8], BF16)
        inv_sb = kept("inv_sb", [P, PIX], BF16)
        x_sb = [kept("x_sb%d" % i, [P, PIX], BF16) for i in range(TILES)]
        meas = [[kept("meas%d_%d" % (i, j), [P, 1024], BF16) for j in range(2)] for i in range(TILES)]
        f_raw_words = [kept("f_raw_words%d" % g, [P, PIX_GROUPS, 1024], U8) for g in range(BIN_GROUPS)]
        f_raw_scales = [kept("f_raw_scales%d" % j, [P, PIX_GROUPS, n * K_PASS], U8) for j, n in enumerate((1, 3))]
        f_words = [kept("f_words%d" % g, [P, 2, PIX_GROUPS, 2, 2 * P], U8) for g in range(BIN_GROUPS)]
        f_scales = [kept("f_scales%d" % g, [P, 2, PIX_GROUPS, 2, P], U8) for g in range(BIN_GROUPS)]
        g_words = [kept("g_words%d" % g, [P, 2 * PIX], U8) for g in range(BIN_GROUPS)]
        g_scales = [kept("g_scales%d" % j, [P, 2, PIX], U8) for j in range(2)]
        x_codes = kept("x_codes", [P, PIX_GROUPS, M], U32)
        x_scales = kept("x_scales", [P, PIX_GROUPS, M], U8)
        roots = [kept("roots%d" % g, [P, 4, M], F32) for g in range(BIN_GROUPS)]
        recips = [kept("recips%d" % g, [P, 2, M, 2], F32) for g in range(BIN_GROUPS)]
        r_codes = [kept("r_codes%d" % g, [P, M], U32) for g in range(BIN_GROUPS)]
        r_scales = [kept("r_scales%d" % g, [P, M], U8) for g in range(BIN_GROUPS)]
        y_sb = [kept("y_sb%d" % i, [P, PIX], F32) for i in range(TILES)]
        y_codes = kept("y_codes", [P, PIX_GROUPS, M], U32)
        y_scales = kept("y_scales", [P, PIX_GROUPS, M], U8)

        def images(first, count):
            return slice(P * first, P * (first + count))

        def load_x(i):
            nc.sync.dma_start(out=x_sb[i][:], in_=x[images(i, 1), :])

        def load_x_half(i, k):
            cols = slice(K_PASS * k, K_PASS * (k + 1))
            nc.sync.dma_start(out=x_sb[i][:, cols], in_=x[images(i, 1), cols])

        def load_meas(i, j):
            nc.sync.dma_start(out=meas[i][j][:], in_=measured[images(i, 1), 1024 * j : 1024 * (j + 1)])

        def load_f(g):
            src = fwd_words[:, :, 1024 * g : 1024 * (g + 1)].rearrange("g p n -> p g n")
            nc.sync.dma_start(out=f_raw_words[g][:].bitcast(I32), in_=src.bitcast(I32))

        def load_g(g):
            nc.sync.dma_start(out=g_words[g][:].bitcast(I32), in_=back_words[g].bitcast(I32))

        def load_scales(plane, rows):
            for q in range(4):
                src = rows[:, 4 * q : 4 * q + 4, :].rearrange("g r n -> r g n")
                nc.sync.dma_start(out=plane[32 * q : 32 * q + 4, :, :].bitcast(I32), in_=src.bitcast(I32))

        def move(eng, out, in_):
            if eng is A:
                nc.scalar.copy(out=out, in_=in_)
            else:
                eng.tensor_copy(out=out, in_=in_)

        def bank(role, shape):
            bufs = {"turn": 2, "expected": 2}.get(role, 1)
            return psum.tile(shape, F32, name=role, tag=role, bufs=bufs)

        def inv_turn():
            turned = bank("turn", [P, 4, P])
            words = inv_col[:].bitcast(F32)
            for j in range(4):
                nc.tensor.transpose(turned[:, j, :], words[:, j : j + 1].to_broadcast([P, P]), ident[:])
            live["inv"] = turned

        def inv_copy(eng):
            move(eng, inv_sb[:].bitcast(F32).rearrange("p (n j) -> p n j", j=4), live["inv"][:].rearrange("p j n -> p n j"))

        def x_turn(i, ks):
            turned = bank("back%d" % i if ks[0] == 0 else "turn", [P, 4, P])
            words = x_sb[i][:].bitcast(F32)
            for n, k in enumerate(ks):
                for u in range(2):
                    nc.tensor.transpose(turned[:, 2 * n + u, :], words[:, 2 * P * k + u : 2 * P * (k + 1) : 2], ident[:])
            live["xT", i, ks[0]] = turned

        def interleave(turned, groups, name, eng):
            grouped = work.tile([P, 1024], BF16, name=name, bufs=5, align_bytes=64)
            move(
                eng,
                grouped[:, : K_PASS * groups].bitcast(F32).rearrange("p (g m u) -> p g m u", g=groups, u=2),
                turned[:, : 2 * groups, :].rearrange("p (g u) m -> p g m u", u=2),
            )
            return grouped

        def x_copy(i, ks, eng):
            grouped = interleave(live["xT", i, ks[0]], len(ks), "x_grouped", eng)
            for n, k in enumerate(ks):
                live["xg", i, k] = grouped[:, K_PASS * n : K_PASS * (n + 1)]

        def x_quant(i, k):
            nc.vector.quantize_mx(
                out=x_codes[:, k, images(i, 1)].bitcast(FP8X4),
                scales=x_scales[:, k, images(i, 1)],
                in_=live["xg", i, k],
            )

        def scale_x(i, hs, eng):
            cols = slice(K_PASS * hs[0], K_PASS * (hs[-1] + 1))
            xs = kept("xs%d_%d" % (i, hs[0]), [P, K_PASS * len(hs)], F32)
            eng.tensor_tensor(out=xs[:], in0=x_sb[i][:, cols], in1=inv_sb[:, cols], op=ALU.mult)
            for a, h in enumerate(hs):
                live["xs", i, h] = xs[:, K_PASS * a : K_PASS * (a + 1)]

        def sort_words(g, u):
            nc.vector.tensor_copy(
                out=f_words[g][:, u, :, :, :].rearrange("p k e (n b) -> p k e n b", b=2),
                in_=f_raw_words[g][:].rearrange("p k (n u e b) -> p u k e n b", u=2, e=2, b=2)[:, u, :, :, :, :],
            )

        def sort_scales(g, us):
            raw = f_raw_scales[min(g, 1)][:, :, K_PASS * max(g - 1, 0) : K_PASS * max(g, 1)]
            picked = slice(us[0], us[-1] + 1)
            nc.vector.tensor_copy(
                out=f_scales[g][:, picked, :, :, :],
                in_=raw.rearrange("p k (n u e) -> p u k e n", u=2, e=2)[:, picked, :, :, :],
            )

        def project(g, first, count, j, part=None):
            slots = 4 // count
            part = part or range(slots)
            if part[0] == 0:
                live["e", g, first, j] = bank("expected", [P, slots, P * count])
            expected = live["e", g, first, j]
            runs = [(first, count)] if count == TILES else [(i, 1) for i in range(first, first + count)]
            for s in part:
                u, e = divmod(slots * j + s, 2)
                for i, n in runs:
                    for k in range(PIX_GROUPS):
                        nc.tensor.matmul_mx(
                            out=expected[:, s, images(i - first, n)],
                            lhsT=f_words[g][:, u, k, e, :].bitcast(FP4X4),
                            lhsT_scale=f_scales[g][:, u, k, e, :],
                            rhs=x_codes[:, k, images(i, n)].bitcast(FP8X4),
                            rhs_scale=x_scales[:, k, images(i, n)],
                            start=(k == 0),
                            stop=(k == PIX_GROUPS - 1),
                        )

        def rsqrt(g, first, count, j):
            slots = 4 // count
            for s in range(slots):
                t = slots * j + s
                nc.scalar.activation(
                    out=roots[g][:, t, images(first, count)],
                    in_=live["e", g, first, j][:, s, :],
                    func=ACT.Abs_reciprocal_sqrt,
                    bias=bg_col[:, g, t : t + 1],
                )

        def square(g, first, count, us, eng):
            picked = slice(us[0], us[-1] + 1)
            src = roots[g][:, :, images(first, count)].rearrange("p (u e) m -> p u m e", e=2)[:, picked, :, :]
            dst = recips[g][:, picked, images(first, count), :]
            if eng is A:
                nc.scalar.activation(out=dst, in_=src, func=ACT.Square)
            else:
                eng.tensor_tensor(out=dst, in0=src, in1=src, op=ALU.mult)

        def meas_turn(g, half):
            turned = bank("turn", [P, 2, 2 * P])
            for a in range(2):
                words = meas[2 * half + a][g // 2][:].bitcast(F32)
                for u in range(2):
                    start = 2 * P * (g % 2)
                    nc.tensor.transpose(turned[:, u, images(a, 1)], words[:, start + u : start + 2 * P : 2], ident[:])
            live["mT", g, half] = turned

        def times_measured(g, first, count):
            ratio = kept("ratio%d_%d" % (g, first), [P, K_PASS * count], BF16)
            turned = live["mT", g, first // 2][:].bitcast(BF16).rearrange("p u (m e) -> p m u e", e=2)
            nc.vector.tensor_tensor(
                out=ratio[:].rearrange("p (m u e) -> p m u e", u=2, e=2),
                in0=recips[g][:, :, images(first, count), :].rearrange("p u m e -> p m u e"),
                in1=turned[:, images(first % 2, count), :, :],
                op=ALU.mult,
            )
            live["ratio", g, first] = ratio

        def ratio_quant(g, first, count):
            nc.vector.quantize_mx(
                out=r_codes[g][:, images(first, count)].bitcast(FP8X4),
                scales=r_scales[g][:, images(first, count)],
                in_=live["ratio", g, first][:],
            )

        def back_project(i, g, h):
            if g == 0:
                live["b", i, h] = bank(back_banks[i][h], [P, K_PASS])
            nc.tensor.matmul_mx(
                out=live["b", i, h][:],
                lhsT=r_codes[g][:, images(i, 1)].bitcast(FP8X4),
                lhsT_scale=r_scales[g][:, images(i, 1)],
                rhs=g_words[g][:, 1024 * h : 1024 * (h + 1)].bitcast(FP4X4),
                rhs_scale=g_scales[g // 2][:, g % 2, K_PASS * h : K_PASS * (h + 1)],
                start=(g == 0),
                stop=(g == BIN_GROUPS - 1),
            )

        def update(i, h):
            cols = slice(K_PASS * h, K_PASS * (h + 1))
            nc.vector.tensor_tensor(out=y_sb[i][:, cols], in0=live["b", i, h][:], in1=live["xs", i, h], op=ALU.mult)
            nc.sync.dma_start(out=out_0[images(i, 1), cols], in_=y_sb[i][:, cols])

        def y_round(i, hs, eng):
            for h in hs:
                yb = work.tile([P, K_PASS], BF16, name="y_bf16", bufs=8)
                move(eng, as_uqe(yb[:]), pairs_apart(y_sb[i][:, K_PASS * h : K_PASS * (h + 1)]))
                live["yb", i, h] = yb

        def y_direct(i, h):
            yb = work.tile([P, K_PASS], BF16, name="y_bf16", bufs=8)
            nc.vector.tensor_tensor(
                out=as_uqe(yb[:]), in0=pairs_apart(live["b", i, h][:]), in1=pairs_apart(live["xs", i, h]), op=ALU.mult
            )
            live["yb", i, h] = yb

        def y_turn(i, hs):
            turned = bank("turn", [P, 4, P])
            for n, h in enumerate(hs):
                words = live["yb", i, h][:].bitcast(F32)
                for u in range(2):
                    nc.tensor.transpose(turned[:, 2 * n + u, :], words[:, P * u : P * (u + 1)], ident[:])
            live["yT", i, hs[0]] = turned

        def y_copy(i, hs, eng):
            grouped = interleave(live["yT", i, hs[0]], len(hs), "y_grouped", eng)
            for a, h in enumerate(hs):
                live["yg", i, h] = grouped[:, K_PASS * a : K_PASS * (a + 1)]

        def y_quant(i, h):
            nc.vector.quantize_mx(
                out=y_codes[:, h, images(i, 1)].bitcast(FP8X4), scales=y_scales[:, h, images(i, 1)], in_=live["yg", i, h]
            )

        def store_words(i, hs):
            picked = slice(hs[0], hs[-1] + 1)
            dst = out_1[picked, :, images(i, 1), :].rearrange("g p m t -> p g (m t)")
            nc.sync.dma_start(out=dst.bitcast(I32), in_=y_codes[:, picked, images(i, 1)].bitcast(I32))

        def store_scales():
            for q in range(4):
                eng = nc.sync if q % 2 == 0 else nc.scalar
                dst = out_2[:, 4 * q : 4 * q + 4, :].rearrange("g r m -> r g m")
                eng.dma_start(out=dst.bitcast(I32), in_=y_scales[32 * q : 32 * q + 4, :, :].bitcast(I32))

        def clear(eng, plane):
            eng.memset(plane[:].rearrange("p g n -> p (g n)").bitcast(I32), 0)

        clear(V, f_raw_scales[0])
        nc.vector.memset(warm_in[:], 1.0)
        make_identity(nc, ident[:])
        nc.scalar.activation(out=warm_out[:], in_=warm_in[:], func=ACT.Abs_reciprocal_sqrt)
        clear(V, f_raw_scales[1])
        clear(V, g_scales[0])
        clear(V, g_scales[1])
        load_x_half(0, 0)
        load_x_half(0, 1)
        load_f(0)
        load_x(1)
        load_scales(f_raw_scales[0], fwd_scales[:, :, :K_PASS])
        nc.sync.dma_start(out=bg_col[:], in_=background.rearrange("(c p t) -> p c t", p=P, t=4))
        load_x(2)
        load_x(3)
        load_scales(f_raw_scales[1], fwd_scales[:, :, K_PASS:])
        load_f(1)
        load_meas(0, 0)
        load_meas(1, 0)
        nc.sync.dma_start(out=inv_col[:], in_=inv_sens.rearrange("(p t) -> p t", t=8))
        load_meas(2, 0)
        load_meas(3, 0)
        load_scales(g_scales[0], back_scales[0:2])
        load_g(0)
        load_f(2)
        load_g(1)
        load_meas(0, 1)
        load_meas(1, 1)
        load_f(3)
        load_meas(2, 1)
        load_meas(3, 1)
        load_scales(g_scales[1], back_scales[2:4])
        load_g(2)
        load_g(3)

        x_turn(0, [0])
        x_turn(0, [1])
        x_copy(0, [0], A)
        sort_words(0, 0)
        x_copy(0, [1], A)
        x_turn(1, [0, 1])
        x_quant(0, 0)
        x_quant(0, 1)
        sort_scales(0, [0])
        sort_scales(0, [1])
        x_turn(2, [0, 1])
        x_copy(1, [0, 1], A)
        sort_words(0, 1)
        x_quant(1, 0)
        x_quant(1, 1)
        project(0, 0, 1, 0, [0, 1])
        x_copy(2, [0, 1], A)
        sort_scales(1, [0, 1])
        project(0, 0, 1, 0, [2, 3])
        x_quant(2, 0)
        x_quant(2, 1)
        project(0, 1, 1, 0)
        sort_words(1, 0)
        rsqrt(0, 0, 1, 0)
        sort_words(1, 1)
        x_turn(3, [0, 1])
        square(0, 0, 1, [0, 1], A)
        sort_scales(3, [0, 1])
        project(0, 2, 1, 0)
        rsqrt(0, 1, 1, 0)
        x_copy(3, [0, 1], V)
        meas_turn(0, 0)
        square(0, 1, 1, [0, 1], A)
        inv_turn()
        x_quant(3, 0)
        rsqrt(0, 2, 1, 0)
        x_quant(3, 1)
        times_measured(0, 0, 1)
        project(0, 3, 1, 0)
        square(0, 2, 1, [0, 1], A)
        times_measured(0, 1, 1)
        project(1, 0, 4, 1)
        ratio_quant(0, 0, 1)
        rsqrt(0, 3, 1, 0)
        sort_scales(2, [0, 1])
        meas_turn(0, 1)
        rsqrt(1, 0, 4, 1)
        ratio_quant(0, 1, 1)
        sort_words(2, 0)
        project(1, 0, 4, 0)
        square(0, 3, 1, [0, 1], A)
        inv_copy(V)
        project(1, 0, 4, 2)
        rsqrt(1, 0, 4, 0)
        sort_words(2, 1)
        back_project(0, 0, 1)
        rsqrt(1, 0, 4, 2)
        back_project(0, 0, 0)
        back_project(1, 0, 1)
        times_measured(0, 2, 1)
        scale_x(3, [0], G)
        project(1, 0, 4, 3)
        square(1, 0, 4, [0], A)
        times_measured(0, 3, 1)
        project(2, 0, 2, 1)
        rsqrt(1, 0, 4, 3)
        ratio_quant(0, 3, 1)
        meas_turn(1, 1)
        sort_words(3, 0)
        rsqrt(2, 0, 2, 1)
        meas_turn(1, 0)
        sort_words(3, 1)
        square(1, 0, 4, [1], A)
        project(2, 0, 2, 0)
        scale_x(3, [1], V)
        project(3, 0, 2, 0)
        ratio_quant(0, 2, 1)
        rsqrt(2, 0, 2, 0)
        scale_x(1, [0], G)
        times_measured(1, 2, 2)
        back_project(1, 0, 0)
        rsqrt(3, 0, 2, 0)
        project(3, 0, 2, 1)
        square(2, 0, 2, [0], A)
        times_measured(1, 0, 2)
        scale_x(2, [1], G)
        project(2, 2, 2, 1)
        rsqrt(3, 0, 2, 1)
        meas_turn(2, 0)
        square(2, 0, 2, [1], A)
        ratio_quant(1, 0, 2)
        meas_turn(3, 0)
        ratio_quant(1, 2, 2)
        square(3, 0, 2, [1], A)
        project(2, 2, 2, 0)
        times_measured(2, 0, 2)
        scale_x(0, [0], G)
        square(3, 0, 2, [0], A)
        back_project(1, 1, 0)
        rsqrt(2, 2, 2, 1)
        back_project(0, 1, 1)
        times_measured(3, 0, 2)
        back_project(1, 1, 1)
        back_project(0, 1, 0)
        rsqrt(2, 2, 2, 0)
        project(3, 2, 1, 0)
        square(2, 2, 2, [1], A)
        ratio_quant(2, 0, 2)
        meas_turn(2, 1)
        scale_x(0, [1], V)
        square(2, 2, 2, [0], A)
        ratio_quant(3, 0, 2)
        meas_turn(3, 1)
        rsqrt(3, 2, 1, 0)
        scale_x(1, [1], G)
        times_measured(2, 2, 2)
        back_project(0, 2, 1)
        back_project(0, 3, 1)
        square(3, 2, 1, [0, 1], A)
        project(3, 3, 1, 0)
        update(0, 1)
        back_project(0, 2, 0)
        rsqrt(3, 3, 1, 0)
        back_project(0, 3, 0)
        ratio_quant(2, 2, 2)
        back_project(1, 2, 1)
        scale_x(2, [0], G)
        update(0, 0)
        back_project(1, 2, 0)
        y_round(0, [1], A)
        back_project(1, 3, 0)
        times_measured(3, 2, 1)
        back_project(2, 0, 1)
        y_round(0, [0], A)
        back_project(1, 3, 1)
        update(1, 0)
        back_project(2, 1, 1)
        square(3, 3, 1, [0, 1], A)
        back_project(2, 0, 0)
        ratio_quant(3, 2, 1)
        back_project(2, 2, 1)
        update(1, 1)
        y_round(1, [0], A)
        back_project(2, 1, 0)
        back_project(3, 0, 0)
        times_measured(3, 3, 1)
        back_project(2, 3, 1)
        y_round(1, [1], A)
        back_project(2, 2, 0)
        update(2, 1)
        back_project(2, 3, 0)
        y_turn(0, [0, 1])
        ratio_quant(3, 3, 1)
        update(2, 0)
        y_turn(1, [0, 1])
        y_copy(0, [0, 1], A)
        back_project(3, 1, 0)
        y_round(2, [1], V)
        back_project(3, 2, 0)
        y_copy(1, [0, 1], A)
        y_quant(0, 0)
        back_project(3, 3, 0)
        back_project(3, 0, 1)
        y_round(2, [0], A)
        update(3, 0)
        back_project(3, 1, 1)
        back_project(3, 2, 1)
        y_quant(1, 0)
        back_project(3, 3, 1)
        y_quant(1, 1)
        store_words(1, [0, 1])
        y_round(3, [0], A)
        y_quant(0, 1)
        store_words(0, [0, 1])
        y_turn(2, [0, 1])
        y_direct(3, 1)
        y_copy(2, [0, 1], A)
        update(3, 1)
        y_turn(3, [1])
        y_copy(3, [1], A)
        y_turn(3, [0])
        y_quant(2, 0)
        y_quant(2, 1)
        store_words(2, [0, 1])
        y_copy(3, [0], A)
        y_quant(3, 1)
        store_words(3, [1])
        y_quant(3, 0)
        store_words(3, [0])
        store_scales()
